import numpy as np
import ml_dtypes


def mxq(x, axis, fmt="e4m3"):
    dtype, down = {"e4m3": (ml_dtypes.float8_e4m3fn, 7), "e5m2": (ml_dtypes.float8_e5m2, 14)}[fmt]
    v = np.moveaxis(np.asarray(x, np.float32).astype(ml_dtypes.bfloat16).astype(np.float64), axis, -1)
    blocks = v.reshape(v.shape[:-1] + (-1, 32))
    amax = np.abs(blocks).max(-1, keepdims=True)
    byte = np.maximum(np.where(amax > 0, np.frexp(amax)[1] - 1 + 127, 0) - down, 1)
    scale = np.exp2(byte - 127.0)
    codes = (blocks / scale).astype(np.float32).astype(dtype).astype(np.float64)
    return np.moveaxis((codes * scale).reshape(v.shape), -1, axis)


WIDE = False


def mx_kscale(k):
    if not WIDE:
        return np.ones(k)
    levels = np.array([10, -10, 5, -5, 0])
    if k % 512:
        return np.exp2(np.random.permutation(np.resize(levels, k // 32))).repeat(32)
    a = np.empty((k // 512, 16))
    for p in range(k // 512):
        a[p, :8] = np.random.permutation(np.resize(levels, 8))
        for g in range(8):
            far = levels[np.abs(levels - a[p, g]) >= 10]
            a[p, g + 8] = far[np.random.randint(len(far))]
    return np.exp2(a.ravel()).repeat(32)


BF16 = ml_dtypes.bfloat16


def bf(x):
    return np.asarray(x, np.float32).astype(BF16)


def f64(x):
    return np.asarray(x).astype(np.float64)


E2M1 = np.array([0.0, 0.5, 1.0, 1.5, 2.0, 3.0, 4.0, 6.0, -0.0, -0.5, -1.0, -1.5, -2.0, -3.0, -4.0, -6.0])


def pack_weight(w, fmt):
    k, n = w.shape
    w = f64(bf(w)).reshape(k // 32, 32, n)
    amax = np.abs(w).max(1)
    if fmt == "e4m3":
        byte = np.frexp(amax)[1] - 1 + 127 - 7
    else:
        mant, ex = np.frexp(amax / 6.0)
        byte = np.where(mant > 0.5, ex, ex - 1) + 127
    byte = np.clip(np.where(amax > 0, byte, 1), 1, 254)
    scaled = (w * np.exp2(127.0 - byte)[:, None, :]).reshape(k, n).astype(np.float32)
    by_word = np.ascontiguousarray(scaled.reshape(k // 512, 128, 4, n).transpose(0, 1, 3, 2))
    if fmt == "e4m3":
        words = by_word.astype(ml_dtypes.float8_e4m3fn).view(np.uint8)
    else:
        c = by_word.astype(ml_dtypes.float4_e2m1fn).view(np.uint8) & 0xF
        words = c[..., 0::2] | (c[..., 1::2] << 4)
    return np.ascontiguousarray(words), np.ascontiguousarray(byte.astype(np.uint8).reshape(k // 512, 16, n))


def unpack_weight(words, scales, fmt):
    g, p, n, _ = words.shape
    if fmt == "e4m3":
        vals = np.ascontiguousarray(words).view(ml_dtypes.float8_e4m3fn).astype(np.float64)
    else:
        nib = np.empty((g, p, n, 4), np.uint8)
        nib[..., 0::2] = words & 0xF
        nib[..., 1::2] = words >> 4
        vals = E2M1[nib]
    vals = vals * np.repeat(np.exp2(scales.astype(np.float64) - 127.0), 8, axis=1)[..., None]
    return vals.transpose(0, 1, 3, 2).reshape(g * 512, n)
def pack4(w):
    words, scales = pack_weight(w, "e2m1")
    return words.reshape(words.shape[0], 128, -1), scales


def unpack4(words, scales):
    return unpack_weight(words.reshape(words.shape[0], 128, -1, 2), scales, "e2m1")


def planes(Y):
    n, m = Y.shape
    b = f64(bf(Y)).reshape(n // 32, 32, m)
    amax = np.abs(b).max(1)
    byte = np.clip(np.where(amax > 0, np.frexp(amax)[1] - 1 + 127 - 7, 1), 1, 254)
    codes = (b * np.exp2(127.0 - byte)[:, None, :]).reshape(n, m).astype(np.float32).astype(ml_dtypes.float8_e4m3fn).view(np.uint8)
    words = codes.reshape(n // 512, 128, 4, m).transpose(0, 1, 3, 2)
    return np.ascontiguousarray(words), np.ascontiguousarray(byte.astype(np.uint8).reshape(n // 512, 16, m))


M, K, A, N = 1024, 2048, 1024, 2048


def setup_inputs():
    s = mx_kscale(K)
    t = mx_kscale(A)
    flow = np.random.randn(K, M) * s[:, None]
    decay = 1.5 / np.sqrt(1.0 + 3.0 * np.arange(K) / K)
    impact = np.random.randn(K, A) / np.sqrt(K) * decay[:, None] / s[:, None]
    flow_words, flow_scales = pack_weight(flow, "e4m3")
    impact_words, impact_scales = pack4(impact)
    depth_gain = np.exp(0.3 * np.random.randn(A)) * t
    response = np.random.randn(A, N) / np.sqrt(A) / t[:, None]
    drift = 0.3 * np.random.randn(N)
    schedule = np.exp(0.8 * np.random.randn(N))[None, :] * np.exp(0.3 * np.random.randn(M, N))
    return {"flow_words": flow_words, "flow_scales": flow_scales,
            "impact_words": impact_words, "impact_scales": impact_scales,
            "depth_gain": bf(depth_gain), "response": bf(response),
            "drift": bf(drift), "schedule": bf(schedule)}


def reference(flow_words, flow_scales, impact_words, impact_scales, depth_gain, response, drift, schedule):
    X = unpack_weight(flow_words, flow_scales, "e4m3")
    G = unpack4(impact_words, impact_scales)
    U = X.T @ G
    H = np.sign(U) * np.abs(U) ** (1.0 / 3.0) * f64(depth_gain)
    D = mxq(H, 1, "e4m3") @ mxq(f64(response), 0, "e4m3")
    y = (D + f64(drift)) * f64(schedule)
    words, scales = planes(y.T)
    return y, words, scales

@@ -1,0 +1,420 @@
+from contextlib import ExitStack
+
+import concourse.mybir as mybir
+from concourse.masks import make_identity
+
+M, K, A, N = 1024, 2048, 1024, 2048
+FLOPS = 2 * M * K * A + 2 * M * A * N
+
+F32 = mybir.dt.float32
+BF16 = mybir.dt.bfloat16
+I32 = mybir.dt.int32
+U32 = mybir.dt.uint32
+U8 = mybir.dt.uint8
+FP8X4 = mybir.dt.float8_e4m3fn_x4
+FP4X4 = mybir.dt.float4_e2m1fn_x4
+ACT = mybir.ActivationFunctionType
+ALU = mybir.AluOpType
+
+P = 128
+W = 512
+LN_FLOOR = 2.0 ** -60
+CAST = ["v"] * 5 + ["sv"] * 4 + ["v"] * 3
+ROT = (9, 10, 0, 1, 2, 3)
+UNITS = [(0, 256, 0), (0, 256, 1), (256, 256, 0), (256, 256, 1), (0, 512, 2), (0, 512, 3)] + [(512, 512, q) for q in range(3)] + [(512, 256, 3), (768, 128, 3), (896, 128, 3)]
+X_CHUNKS = ((0, 256), (256, 512), (512, 1024))
+
+
+def tile_cube_root_impact_cost_h2_kernel(
+    tc, flow_words, flow_scales, impact_words, impact_scales, depth_gain, response, drift, schedule,
+    out_0, out_1, out_2,
+):
+    nc = tc.nc
+    with ExitStack() as ctx:
+        keep = ctx.enter_context(tc.tile_pool(name="keep", bufs=1))
+        flow = ctx.enter_context(tc.tile_pool(name="flow", bufs=2))
+        psum = ctx.enter_context(tc.psum_pool(name="psum", bufs=1))
+        ctx.enter_context(tc.manual_schedule())
+
+        banks_taken = []
+
+        def bank():
+            n = len(banks_taken)
+            tile = psum.tile([P, W], F32, name="bank%d" % n, tag="bank%d" % (n % 8))
+            banks_taken.append(tile)
+            return tile
+
+        def big(shape, dtype, slot, name):
+            return keep.tile(shape, dtype, name=name, tag="big%d" % slot, align_bytes=64)
+
+        def small(shape, dtype, slot, name):
+            return keep.tile(shape, dtype, name=name, tag="small%d" % slot, align_bytes=64)
+
+        x_scales = keep.tile([P, 4, M], U8, name="x_scales", align_bytes=64)
+        g_scales = keep.tile([P, 4, A], U8, name="g_scales", align_bytes=64)
+        nc.vector.memset(g_scales[:].bitcast(I32), 0)
+        nc.vector.memset(x_scales[:].bitcast(I32), 0)
+        ident = keep.tile([P, P], F32, name="ident")
+        make_identity(nc, ident[:])
+        warm = keep.tile([P, 1], F32, name="warm")
+        nc.scalar.activation(out=warm[:], in_=ident[:, 0:1], func=ACT.Ln, bias=1.0)
+
+        g_words = []
+        x_words = []
+
+        def load_g(half):
+            tile = small([P, 4, 2 * W], U8, half, "g_words%d" % half)
+            nc.sync.dma_start(
+                out=tile[:].bitcast(I32),
+                in_=impact_words[:, :, 2 * W * half : 2 * W * (half + 1)].rearrange("g p b -> p g b").bitcast(I32),
+            )
+            g_words.append(tile)
+
+        def load_x(c):
+            m0, m1 = X_CHUNKS[c]
+            if m1 - m0 == W:
+                tile = big([P, 4, W], U32, 8, "x_words%d" % c)
+            else:
+                tile = small([P, 4, m1 - m0], U32, 2 + c, "x_words%d" % c)
+            nc.sync.dma_start(
+                out=tile[:].bitcast(I32),
+                in_=flow_words[:, :, m0:m1, :].rearrange("g p m t -> p g (m t)").bitcast(I32),
+            )
+            x_words.append(tile)
+
+        def load_scales(queue, plane, scales, quadrant):
+            queue.dma_start(
+                out=plane[32 * quadrant : 32 * quadrant + 4, :, :].bitcast(I32),
+                in_=scales[:, 4 * quadrant : 4 * quadrant + 4, :].rearrange("g r n -> r g n").bitcast(I32),
+            )
+
+        gain_pairs = keep.tile([P, 2, 4], BF16, name="gain_pairs")
+        nc.sync.dma_start(out=gain_pairs[:], in_=depth_gain.rearrange("(g p t) -> p g t", g=2, t=4))
+        load_g(0)
+        load_x(0)
+        for q in range(4):
+            load_scales(nc.sync, g_scales, impact_scales, q)
+        for q in range(4):
+            load_scales(nc.sync, x_scales, flow_scales, q)
+        load_g(1)
+        load_x(1)
+
+        r_raw = {}
+
+        def load_r(g, nh):
+            tile = big([P, 4, 2 * W], BF16, 9 + 2 * nh + g, "r_raw%d%d" % (g, nh))
+            nc.sync.dma_start(
+                out=tile[:],
+                in_=response[W * g : W * (g + 1), 2 * W * nh : 2 * W * (nh + 1)].rearrange("(p j) n -> p j n", j=4),
+            )
+            r_raw[g, nh] = tile
+
+        s_tiles = {}
+
+        def load_s(h, nh, slot):
+            tile = big([P, 4, 2 * W], BF16, slot, "s%d%d" % (h, nh))
+            nc.sync.dma_start(
+                out=tile[:],
+                in_=schedule[W * h : W * (h + 1), 2 * W * nh : 2 * W * (nh + 1)].rearrange("(i p) n -> p i n", p=P),
+            )
+            s_tiles[h, nh] = tile
+
+        load_r(0, 0)
+        load_x(2)
+        load_r(1, 0)
+        drift_col = keep.tile([P, 4, 4], BF16, name="drift_col")
+        nc.sync.dma_start(out=drift_col[:], in_=drift.rearrange("(g p t) -> p g t", g=4, t=4))
+        load_r(0, 1)
+        load_r(1, 1)
+        load_s(0, 0, 13)
+        load_s(0, 1, 14)
+        load_s(1, 0, 15)
+
+        gain_all = keep.tile([P, A], BF16, name="gain_all")
+
+        def spread_gain():
+            gb = bank()
+            gain_w = gain_pairs[:].rearrange("p g t -> p (g t)").bitcast(F32)
+            for c in range(4):
+                nc.tensor.transpose(gb[:, P * c : P * (c + 1)], gain_w[:, c : c + 1].to_broadcast([P, P]), ident[:])
+            nc.vector.tensor_copy(out=gain_all[:].bitcast(F32), in_=gb[:])
+
+        mag = {}
+        ug = {}
+        u_banks = {}
+
+        def stage1(i, g):
+            c = [n for n, (m0, m1) in enumerate(X_CHUNKS) if m0 <= P * i < m1][0]
+            col = P * i - X_CHUNKS[c][0]
+            u = bank()
+            for k in range(4):
+                nc.tensor.matmul_mx(
+                    out=u[:],
+                    lhsT=x_words[c][:, k, col : col + P].bitcast(FP8X4),
+                    lhsT_scale=x_scales[:, k, P * i : P * (i + 1)],
+                    rhs=g_words[g][:, k, :].bitcast(FP4X4),
+                    rhs_scale=g_scales[:, k, W * g : W * (g + 1)],
+                    start=(k == 0),
+                    stop=(k == 3),
+                )
+            if g == 0:
+                both = big([P, 2, A], F32, i, "mag_ug%d" % i)
+                mag[i] = both[:, 0, :]
+                ug[i] = both[:, 1, :]
+            u_sorted = u[:].rearrange("m (p u e) -> m u p e", u=2, e=2)
+            cols = slice(W * g, W * (g + 1))
+            nc.scalar.activation(
+                out=mag[i][:, cols].rearrange("m (u p e) -> m u p e", u=2, e=2), in_=u_sorted, func=ACT.Abs
+            )
+            u_banks[i, g] = u_sorted
+
+        def times_gain(i, g):
+            cols = slice(W * g, W * (g + 1))
+            u_sorted = u_banks[i, g]
+            nc.vector.tensor_tensor(
+                out=ug[i][:, cols].rearrange("m (u p e) -> m u p e", u=2, e=2),
+                in0=u_sorted,
+                in1=gain_all[:, cols].rearrange("m (u p e) -> m u p e", u=2, e=2),
+                op=ALU.mult,
+            )
+
+        def log_mag(i):
+            nc.scalar.activation(out=mag[i][:], in_=mag[i][:], func=ACT.Ln, bias=LN_FLOOR)
+
+        def power(i):
+            nc.scalar.activation(out=mag[i][:], in_=mag[i][:], func=ACT.Exp, scale=-2.0 / 3.0)
+
+        h_bf = {}
+        h_t = {}
+        h_codes = keep.tile([P, 2, M], U32, name="h_codes", align_bytes=64)
+        h_scales = keep.tile([P, 2, M], U8, name="h_scales", align_bytes=64)
+
+        def copy_on(eng, dst, src):
+            if eng == "s":
+                nc.scalar.copy(out=dst, in_=src)
+            elif eng == "g":
+                nc.gpsimd.tensor_scalar(out=dst, in0=src, scalar1=1.0, scalar2=0.0, op0=ALU.mult, op1=ALU.add)
+            else:
+                nc.vector.tensor_copy(out=dst, in_=src)
+
+        def h_mul(i):
+            h_bf[i] = flow.tile([P, A], BF16, name="h_bf%d" % i, tag="h_bf")
+            nc.vector.tensor_tensor(out=h_bf[i][:], in0=ug[i][:], in1=mag[i][:], op=ALU.mult)
+
+        def h_turn(i, eng):
+            pair, r = divmod(i, 2)
+            if r == 0:
+                h_t[pair] = flow.tile([P, 2, 2 * P, 4], BF16, name="h_t%d" % pair, tag="h_t", align_bytes=64)
+            b = bank()
+            words = h_bf[i][:].bitcast(F32)
+            for c in range(4):
+                nc.tensor.transpose(b[:, P * c : P * (c + 1)], words[:, P * c : P * (c + 1)], ident[:])
+            dst = h_t[pair][:].bitcast(F32)[:, :, P * r : P * (r + 1), :]
+            copy_on(eng, dst, b[:].rearrange("p (g u m) -> p g m u", g=2, u=2))
+
+        def h_quant(pair):
+            for g in range(2):
+                nc.vector.quantize_mx(
+                    out=h_codes[:, g, 2 * P * pair : 2 * P * (pair + 1)].bitcast(FP8X4),
+                    scales=h_scales[:, g, 2 * P * pair : 2 * P * (pair + 1)],
+                    in_=h_t[pair][:, g, :, :].rearrange("p m t -> p (m t)"),
+                )
+
+        r_codes = keep.tile([P, 2, N], U32, name="r_codes", align_bytes=64)
+        r_scales = keep.tile([P, 2, N], U8, name="r_scales", align_bytes=64)
+        r_grouped = {}
+
+        def r_group(g, q, eng="v"):
+            t = flow.tile([P, W, 4], BF16, name="r_grp%d%d" % (g, q), tag="r_grp", bufs=3, align_bytes=64)
+            src = r_raw[g, q // 2][:, :, W * (q % 2) : W * (q % 2 + 1)].rearrange("p j (c m t) -> p c j m t", m=2, t=4)
+            dst = t[:].rearrange("p (t c m) j -> p c j m t", t=4, m=2)
+            copy_on(eng, dst, src)
+            r_grouped[g, q] = t
+
+        def r_quant(g, q):
+            nc.vector.quantize_mx(
+                out=r_codes[:, g, W * q : W * (q + 1)].bitcast(FP8X4),
+                scales=r_scales[:, g, W * q : W * (q + 1)],
+                in_=r_grouped[g, q][:].rearrange("p n t -> p (n t)"),
+            )
+
+        s_t = {}
+        y_t = {}
+        y_bf = {}
+        y = {}
+        y_scales = keep.tile([P, M], U8, name="y_scales", align_bytes=64)
+        slots_taken = []
+
+        def next_big(shape, name):
+            n = len(slots_taken)
+            slots_taken.append(n)
+            return big(shape, F32, ROT[n % len(ROT)], name)
+
+        def s_turn(un, part, eng):
+            m0, mw, q = UNITS[un]
+            if part == 0:
+                s_t[un] = small([P, 2, mw], F32, un % 4, "s_t%d" % un)
+            w = min(mw, 2 * P)
+            b = bank()
+            for u in range(2):
+                for c in range(w // P):
+                    h, i = divmod((m0 + w * part) // P + c, 4)
+                    words = s_tiles[h, q // 2][:, i, W * (q % 2) : W * (q % 2 + 1)].bitcast(F32)
+                    nc.tensor.transpose(b[:, w * u + P * c : w * u + P * (c + 1)], words[:, u : 2 * P : 2], ident[:])
+            copy_on(eng, s_t[un][:, :, w * part : w * (part + 1)], b[:, 0 : 2 * w].rearrange("p (u m) -> p u m", u=2))
+
+        d_banks = {}
+
+        def product(un, t):
+            m0, mw, q = UNITS[un]
+            per_bank = W // mw
+            if t % per_bank == 0:
+                d_banks[un, t // per_bank] = bank()
+            n0 = W * q + P * t
+            for g in range(2):
+                nc.tensor.matmul_mx(
+                    out=d_banks[un, t // per_bank][:, mw * (t % per_bank) : mw * (t % per_bank + 1)],
+                    lhsT=r_codes[:, g, n0 : n0 + P].bitcast(FP8X4),
+                    lhsT_scale=r_scales[:, g, n0 : n0 + P],
+                    rhs=h_codes[:, g, m0 : m0 + mw].bitcast(FP8X4),
+                    rhs_scale=h_scales[:, g, m0 : m0 + mw],
+                    start=(g == 0),
+                    stop=(g == 1),
+                )
+
+        def times_schedule(un, t):
+            m0, mw, q = UNITS[un]
+            per_bank = W // mw
+            if t == 0:
+                y_t[un] = next_big([P, 4, mw], "y_t%d" % un)
+            u, e = divmod(t, 2)
+            nc.vector.scalar_tensor_tensor(
+                out=y_t[un][:, t, :],
+                in0=d_banks[un, t // per_bank][:, mw * (t % per_bank) : mw * (t % per_bank + 1)],
+                scalar=drift_col[:, q, t : t + 1],
+                in1=s_t[un][:, u, :].bitcast(BF16)[:, e : 2 * mw : 2],
+                op0=ALU.add,
+                op1=ALU.mult,
+            )
+
+        def turn_back(un, i, eng="s"):
+            m0, mw, q = UNITS[un]
+            b = bank()
+            for t in range(4):
+                nc.tensor.transpose(b[:, P * t : P * (t + 1)], y_t[un][:, t, P * i : P * (i + 1)], ident[:])
+            if i == 0:
+                y[un] = next_big([P, mw // P, W], "y%d" % un)
+            copy_on(eng, y[un][:, i, :].rearrange("m (p t) -> m p t", t=4), b[:].rearrange("m (t p) -> m p t", t=4))
+            per_store = min(2, mw // P)
+            if i % per_store == per_store - 1:
+                i0 = i - per_store + 1
+                nc.sync.dma_start(
+                    out=out_0[m0 + P * i0 : m0 + P * (i + 1), W * q : W * (q + 1)].rearrange("(i p) n -> p i n", p=P),
+                    in_=y[un][:, i0 : i + 1, :],
+                )
+
+        def y_round(un, eng="v", part=0, parts=1):
+            m0, mw, q = UNITS[un]
+            if part == 0:
+                y_bf[un] = flow.tile([P, mw, 4], BF16, name="y_bf%d" % un, tag="y_bf", align_bytes=64)
+            cols = slice(mw * part // parts, mw * (part + 1) // parts)
+            copy_on(
+                eng,
+                y_bf[un][:, cols, :].rearrange("p (c i) t -> p c t i", i=4),
+                y_t[un][:, :, cols].rearrange("p t (c i) -> p c t i", i=4),
+            )
+
+        def y_quant(un):
+            m0, mw, q = UNITS[un]
+            codes = flow.tile([P, mw], U32, name="y_codes%d" % un, tag="y_codes", bufs=4, align_bytes=64)
+            nc.vector.quantize_mx(
+                out=codes[:].bitcast(FP8X4),
+                scales=y_scales[4 * q : P, m0 : m0 + mw],
+                in_=y_bf[un][:].rearrange("p m t -> p (m t)"),
+            )
+            nc.sync.dma_start(
+                out=out_1[q, :, m0 : m0 + mw, :].rearrange("p m t -> p (m t)").bitcast(I32),
+                in_=codes[:].bitcast(I32),
+            )
+
+        def store_scales():
+            for quad in range(4):
+                nc.sync.dma_start(
+                    out=out_2[:, 4 * quad : 4 * quad + 4, :].bitcast(I32),
+                    in_=y_scales[32 * quad : 32 * quad + 16, :].bitcast(I32),
+                )
+
+        r_parts = [(g, 2 * nh + k) for nh in range(2) for g in range(2) for k in range(2)]
+        order = [(0, 0), (1, 0), (0, 1), (1, 1)] + [(i, g) for i in range(2, 8) for g in range(2)]
+        spread_gain()
+        for n, (i, g) in enumerate(order):
+            stage1(i, g)
+            times_gain(i, g)
+            if n >= 1:
+                if order[n - 1][1] == 1:
+                    log_mag(order[n - 1][0])
+            if n >= 2 and n % 3 == 2 and n // 3 < 5:
+                r_group(*r_parts[n // 3])
+            if n >= 3 and n % 3 == 0 and n // 3 <= 5:
+                r_quant(*r_parts[n // 3 - 1])
+        log_mag(7)
+        load_s(1, 1, 8)
+
+        def s_turn_unit(un, eng):
+            for part in range(max(1, UNITS[un][1] // (2 * P))):
+                s_turn(un, part, eng)
+
+        s_turn_unit(0, "v")
+        s_turn_unit(1, "v")
+        for i in range(4):
+            power(i)
+        h_mul(0)
+        h_mul(1)
+        h_turn(0, "v")
+        h_mul(2)
+        h_turn(1, "v")
+        h_mul(3)
+        h_quant(0)
+        s_turn_unit(2, "s")
+        h_turn(2, "s")
+        h_turn(3, "s")
+        nu = len(UNITS)
+        v_work = {
+            0: [lambda: r_group(*r_parts[6])],
+            1: [lambda: h_quant(1), lambda: r_quant(*r_parts[6]), lambda: h_mul(4)],
+            2: [lambda: h_mul(5), lambda: r_quant(*r_parts[5])],
+            3: [lambda: h_mul(6), lambda: r_quant(*r_parts[7])],
+            4: [lambda: h_mul(7), lambda: h_quant(2)],
+            5: [lambda: h_quant(3)],
+        }
+        s_work = {
+            0: [lambda: power(4), lambda: r_group(*r_parts[5], "s")],
+            1: [lambda: power(5), lambda: r_group(*r_parts[7], "s")],
+            2: [lambda: power(6)],
+            3: [lambda: power(7)],
+        }
+        for un in range(nu + 2):
+            if un < nu:
+                for t in range(4):
+                    product(un, t)
+            if un >= 2:
+                y_quant(un - 2)
+            if 1 <= un <= nu:
+                if CAST[un - 1] == "sv":
+                    y_round(un - 1, "v", 0, 2)
+                    y_round(un - 1, "s", 1, 2)
+                else:
+                    y_round(un - 1, CAST[un - 1])
+            for f in s_work.get(un, []) + v_work.get(un, []):
+                f()
+            if un < nu:
+                for t in range(4):
+                    times_schedule(un, t)
+            if 1 <= un <= nu:
+                for k in range(UNITS[un - 1][1] // P):
+                    turn_back(un - 1, k)
+            if 1 <= un <= 4:
+                h_turn(un + 3, "s")
+            if un + 3 < nu:
+                s_turn_unit(un + 3, "s")
+        store_scales()

@@ -19,9 +19,20 @@ ALU = mybir.AluOpType
 P = 128
 W = 512
 LN_FLOOR = 2.0 ** -60
-CAST = ["v"] * 5 + ["sv"] * 4 + ["v"] * 3
-ROT = (9, 10, 0, 1, 2, 3)
-UNITS = [(0, 256, 0), (0, 256, 1), (256, 256, 0), (256, 256, 1), (0, 512, 2), (0, 512, 3)] + [(512, 512, q) for q in range(3)] + [(512, 256, 3), (768, 128, 3), (896, 128, 3)]
+R0 = 2
+NR = 6
+YB = 1
+SG = 2
+HL = 2
+VCOPY = ()
+R7E = "v"
+R7 = 0
+HM = ((3, -1), (4, 2), (5, 3), (6, 5), (7, 7))
+SL = (1,) * 8
+GCOLS = [176] * 15 + [64, 0]
+VLAST = 1
+ROT = (0, 1, 13, 2, 3, 14)
+UNITS = [(0, 256, q) for q in range(3)] + [(256, 256, q) for q in range(3)] + [(0, 256, 3), (256, 256, 3)] + [(256 * r, 256, q) for r in (2, 3) for q in range(4)][:-1] + [(768, 128, 3), (896, 128, 3)]
 X_CHUNKS = ((0, 256), (256, 512), (512, 1024))
 
 
@@ -50,10 +61,15 @@ def tile_cube_root_impact_cost_h2_kernel(
         def small(shape, dtype, slot, name):
             return keep.tile(shape, dtype, name=name, tag="small%d" % slot, align_bytes=64)
 
-        x_scales = keep.tile([P, 4, M], U8, name="x_scales", align_bytes=64)
-        g_scales = keep.tile([P, 4, A], U8, name="g_scales", align_bytes=64)
-        nc.vector.memset(g_scales[:].bitcast(I32), 0)
-        nc.vector.memset(x_scales[:].bitcast(I32), 0)
+        x_scales = []
+        g_scales = []
+        for half in range(2):
+            for planes, name in ((g_scales, "g_scales%d"), (x_scales, "x_scales%d")):
+                plane = keep.tile([P, 4, W], U8, name=name % half, align_bytes=64)
+                nc.vector.memset(plane[:].bitcast(I32), 0)
+                planes.append(plane)
+        gain_pairs = keep.tile([P, 2, 4], BF16, name="gain_pairs")
+        nc.gpsimd.dma_start(out=gain_pairs[:], in_=depth_gain.rearrange("(g p t) -> p g t", g=2, t=4))
         ident = keep.tile([P, P], F32, name="ident")
         make_identity(nc, ident[:])
         warm = keep.tile([P, 1], F32, name="warm")
@@ -82,22 +98,14 @@ def tile_cube_root_impact_cost_h2_kernel(
             )
             x_words.append(tile)
 
-        def load_scales(queue, plane, scales, quadrant):
-            queue.dma_start(
-                out=plane[32 * quadrant : 32 * quadrant + 4, :, :].bitcast(I32),
-                in_=scales[:, 4 * quadrant : 4 * quadrant + 4, :].rearrange("g r n -> r g n").bitcast(I32),
-            )
-
-        gain_pairs = keep.tile([P, 2, 4], BF16, name="gain_pairs")
-        nc.sync.dma_start(out=gain_pairs[:], in_=depth_gain.rearrange("(g p t) -> p g t", g=2, t=4))
-        load_g(0)
-        load_x(0)
-        for q in range(4):
-            load_scales(nc.sync, g_scales, impact_scales, q)
-        for q in range(4):
-            load_scales(nc.sync, x_scales, flow_scales, q)
-        load_g(1)
-        load_x(1)
+        def load_scales(planes, scales, half, on_sync=4):
+            for quad in range(4):
+                queue = nc.sync if quad < on_sync else nc.gpsimd
+                rows = scales[:, 4 * quad : 4 * quad + 4, W * half : W * (half + 1)]
+                queue.dma_start(
+                    out=planes[half][32 * quad : 32 * quad + 4, :, :].bitcast(I32),
+                    in_=rows.rearrange("g r n -> r g n").bitcast(I32),
+                )
 
         r_raw = {}
 
@@ -119,15 +127,23 @@ def tile_cube_root_impact_cost_h2_kernel(
             )
             s_tiles[h, nh] = tile
 
+        drift_col = keep.tile([P, 4, 4], BF16, name="drift_col")
+        load_g(0)
+        load_x(0)
+        load_scales(g_scales, impact_scales, 0)
+        load_scales(x_scales, flow_scales, 0, 2)
+        load_x(1)
+        load_g(1)
+        load_scales(g_scales, impact_scales, 1)
         load_r(0, 0)
         load_x(2)
+        load_scales(x_scales, flow_scales, 1)
         load_r(1, 0)
-        drift_col = keep.tile([P, 4, 4], BF16, name="drift_col")
-        nc.sync.dma_start(out=drift_col[:], in_=drift.rearrange("(g p t) -> p g t", g=4, t=4))
         load_r(0, 1)
-        load_r(1, 1)
         load_s(0, 0, 13)
+        load_r(1, 1)
         load_s(0, 1, 14)
+        nc.sync.dma_start(out=drift_col[:], in_=drift.rearrange("(g p t) -> p g t", g=4, t=4))
         load_s(1, 0, 15)
 
         gain_all = keep.tile([P, A], BF16, name="gain_all")
@@ -151,9 +167,9 @@ def tile_cube_root_impact_cost_h2_kernel(
                 nc.tensor.matmul_mx(
                     out=u[:],
                     lhsT=x_words[c][:, k, col : col + P].bitcast(FP8X4),
-                    lhsT_scale=x_scales[:, k, P * i : P * (i + 1)],
+                    lhsT_scale=x_scales[i // 4][:, k, P * (i % 4) : P * (i % 4 + 1)],
                     rhs=g_words[g][:, k, :].bitcast(FP4X4),
-                    rhs_scale=g_scales[:, k, W * g : W * (g + 1)],
+                    rhs_scale=g_scales[g][:, k, :],
                     start=(k == 0),
                     stop=(k == 3),
                 )
@@ -178,8 +194,9 @@ def tile_cube_root_impact_cost_h2_kernel(
                 op=ALU.mult,
             )
 
-        def log_mag(i):
-            nc.scalar.activation(out=mag[i][:], in_=mag[i][:], func=ACT.Ln, bias=LN_FLOOR)
+        def log_mag(i, g):
+            part = mag[i][:, W * g : W * (g + 1)]
+            nc.scalar.activation(out=part, in_=part, func=ACT.Ln, bias=LN_FLOOR)
 
         def power(i):
             nc.scalar.activation(out=mag[i][:], in_=mag[i][:], func=ACT.Exp, scale=-2.0 / 3.0)
@@ -226,8 +243,8 @@ def tile_cube_root_impact_cost_h2_kernel(
 
         def r_group(g, q, eng="v"):
             t = flow.tile([P, W, 4], BF16, name="r_grp%d%d" % (g, q), tag="r_grp", bufs=3, align_bytes=64)
-            src = r_raw[g, q // 2][:, :, W * (q % 2) : W * (q % 2 + 1)].rearrange("p j (c m t) -> p c j m t", m=2, t=4)
-            dst = t[:].rearrange("p (t c m) j -> p c j m t", t=4, m=2)
+            src = r_raw[g, q // 2][:, :, W * (q % 2) : W * (q % 2 + 1)].rearrange("p j (c m t) -> p t c j m", m=2, t=4)
+            dst = t[:].rearrange("p (t c m) j -> p t c j m", t=4, m=2)
             copy_on(eng, dst, src)
             r_grouped[g, q] = t
 
@@ -250,18 +267,33 @@ def tile_cube_root_impact_cost_h2_kernel(
             slots_taken.append(n)
             return big(shape, F32, ROT[n % len(ROT)], name)
 
-        def s_turn(un, part, eng):
-            m0, mw, q = UNITS[un]
-            if part == 0:
-                s_t[un] = small([P, 2, mw], F32, un % 4, "s_t%d" % un)
-            w = min(mw, 2 * P)
+        s_banks = {}
+        s_part = {}
+
+        def s_keep(h, q, part, eng):
+            if h == 0:
+                if part == 0:
+                    s_t[h, q] = small([P, 2, W], F32, q, "s_t%d%d" % (h, q))
+                dst = s_t[h, q][:, :, 2 * P * part : 2 * P * (part + 1)]
+            else:
+                if q == 0:
+                    s_t[h, part] = big([P, 4, 2, 2 * P], F32, 9 + part, "s_t%d%d" % (h, part))
+                dst = s_t[h, part][:, q, :, :]
+            s_part[2 * h + part, q] = dst
+            b = s_banks[h, q, part]
+            copy_on(eng, dst, b[:].rearrange("p (u m) -> p u m", u=2))
+
+        def s_flip(h, q, part):
             b = bank()
+            s_banks[h, q, part] = b
             for u in range(2):
-                for c in range(w // P):
-                    h, i = divmod((m0 + w * part) // P + c, 4)
-                    words = s_tiles[h, q // 2][:, i, W * (q % 2) : W * (q % 2 + 1)].bitcast(F32)
-                    nc.tensor.transpose(b[:, w * u + P * c : w * u + P * (c + 1)], words[:, u : 2 * P : 2], ident[:])
-            copy_on(eng, s_t[un][:, :, w * part : w * (part + 1)], b[:, 0 : 2 * w].rearrange("p (u m) -> p u m", u=2))
+                for c in range(2):
+                    words = s_tiles[h, q // 2][:, 2 * part + c, W * (q % 2) : W * (q % 2 + 1)].bitcast(F32)
+                    nc.tensor.transpose(b[:, P * (2 * u + c) : P * (2 * u + c + 1)], words[:, u : 2 * P : 2], ident[:])
+
+        def s_turn(h, q, part, eng):
+            s_flip(h, q, part)
+            s_keep(h, q, part, eng)
 
         d_banks = {}
 
@@ -292,7 +324,7 @@ def tile_cube_root_impact_cost_h2_kernel(
                 out=y_t[un][:, t, :],
                 in0=d_banks[un, t // per_bank][:, mw * (t % per_bank) : mw * (t % per_bank + 1)],
                 scalar=drift_col[:, q, t : t + 1],
-                in1=s_t[un][:, u, :].bitcast(BF16)[:, e : 2 * mw : 2],
+                in1=s_part[m0 // (2 * P), q][:, u, m0 % (2 * P) : m0 % (2 * P) + mw].bitcast(BF16)[:, e : 2 * mw : 2],
                 op0=ALU.add,
                 op1=ALU.mult,
             )
@@ -313,15 +345,14 @@ def tile_cube_root_impact_cost_h2_kernel(
                     in_=y[un][:, i0 : i + 1, :],
                 )
 
-        def y_round(un, eng="v", part=0, parts=1):
+        def y_round(un, eng, c0, c1):
             m0, mw, q = UNITS[un]
-            if part == 0:
-                y_bf[un] = flow.tile([P, mw, 4], BF16, name="y_bf%d" % un, tag="y_bf", align_bytes=64)
-            cols = slice(mw * part // parts, mw * (part + 1) // parts)
+            if un not in y_bf:
+                y_bf[un] = flow.tile([P, mw, 4], BF16, name="y_bf%d" % un, tag="y_bf", bufs=YB, align_bytes=64)
             copy_on(
                 eng,
-                y_bf[un][:, cols, :].rearrange("p (c i) t -> p c t i", i=4),
-                y_t[un][:, :, cols].rearrange("p t (c i) -> p c t i", i=4),
+                y_bf[un][:, c0:c1, :].rearrange("p (c i) t -> p c t i", i=4),
+                y_t[un][:, :, c0:c1].rearrange("p t (c i) -> p c t i", i=4),
             )
 
         def y_quant(un):
@@ -337,84 +368,98 @@ def tile_cube_root_impact_cost_h2_kernel(
                 in_=codes[:].bitcast(I32),
             )
 
-        def store_scales():
+        def store_scales(m0, m1):
             for quad in range(4):
                 nc.sync.dma_start(
-                    out=out_2[:, 4 * quad : 4 * quad + 4, :].bitcast(I32),
-                    in_=y_scales[32 * quad : 32 * quad + 16, :].bitcast(I32),
+                    out=out_2[:, 4 * quad : 4 * quad + 4, m0:m1].bitcast(I32),
+                    in_=y_scales[32 * quad : 32 * quad + 16, m0:m1].bitcast(I32),
                 )
 
-        r_parts = [(g, 2 * nh + k) for nh in range(2) for g in range(2) for k in range(2)]
-        order = [(0, 0), (1, 0), (0, 1), (1, 1)] + [(i, g) for i in range(2, 8) for g in range(2)]
+        r_parts = [(0, 0), (0, 1), (1, 0), (1, 1), (0, 2), (1, 2), (0, 3), (1, 3)]
+        order = [(i, g) for g in range(2) for i in range(4)] + [(i, g) for i in range(4, 8) for g in range(2)]
         spread_gain()
         for n, (i, g) in enumerate(order):
             stage1(i, g)
             times_gain(i, g)
             if n >= 1:
-                if order[n - 1][1] == 1:
-                    log_mag(order[n - 1][0])
-            if n >= 2 and n % 3 == 2 and n // 3 < 5:
-                r_group(*r_parts[n // 3])
-            if n >= 3 and n % 3 == 0 and n // 3 <= 5:
-                r_quant(*r_parts[n // 3 - 1])
-        log_mag(7)
+                log_mag(*order[n - 1])
+            if n >= R0 and (n - R0) % 2 == 0 and (n - R0) // 2 < NR:
+                r_group(*r_parts[(n - R0) // 2])
+            if n >= R0 and (n - R0) % 2 == 1 and (n - R0) // 2 < NR:
+                r_quant(*r_parts[(n - R0) // 2])
+        log_mag(*order[-1])
         load_s(1, 1, 8)
-
-        def s_turn_unit(un, eng):
-            for part in range(max(1, UNITS[un][1] // (2 * P))):
-                s_turn(un, part, eng)
-
-        s_turn_unit(0, "v")
-        s_turn_unit(1, "v")
-        for i in range(4):
-            power(i)
+        early = [(0, q, part) for part in range(2) for q in range(3)]
+        s_left = [(0, 3, 0), (0, 3, 1)] + [(1, q, part) for part in range(2) for q in range(4)]
+        for args in early:
+            s_flip(*args)
+        s_keep(*early[0], "v")
+        s_keep(*early[1], "v")
+        power(0)
+        power(1)
         h_mul(0)
+        s_keep(*early[2], "s")
+        s_keep(*early[3], "s")
         h_mul(1)
         h_turn(0, "v")
-        h_mul(2)
+        power(2)
         h_turn(1, "v")
-        h_mul(3)
+        s_keep(*early[4], "s")
+        s_keep(*early[5], "s")
+        power(3)
+        h_mul(2)
         h_quant(0)
-        s_turn_unit(2, "s")
-        h_turn(2, "s")
-        h_turn(3, "s")
+        for args in s_left[:SG]:
+            s_turn(*args, "s")
+        for t in range(4):
+            product(0, t)
+        power(4)
+        r_group(*r_parts[6], "s")
         nu = len(UNITS)
-        v_work = {
-            0: [lambda: r_group(*r_parts[6])],
-            1: [lambda: h_quant(1), lambda: r_quant(*r_parts[6]), lambda: h_mul(4)],
-            2: [lambda: h_mul(5), lambda: r_quant(*r_parts[5])],
-            3: [lambda: h_mul(6), lambda: r_quant(*r_parts[7])],
-            4: [lambda: h_mul(7), lambda: h_quant(2)],
-            5: [lambda: h_quant(3)],
-        }
-        s_work = {
-            0: [lambda: power(4), lambda: r_group(*r_parts[5], "s")],
-            1: [lambda: power(5), lambda: r_group(*r_parts[7], "s")],
-            2: [lambda: power(6)],
-            3: [lambda: power(7)],
-        }
-        for un in range(nu + 2):
-            if un < nu:
+        v_work = {}
+        s_work = {}
+        h_turn_at = {}
+        for i, un in HM:
+            v_work.setdefault(un, []).append(lambda i=i: h_mul(i))
+            h_turn_at.setdefault(un + 1, []).append(i)
+            if i > 4:
+                s_work.setdefault(un - 1, []).append(lambda i=i: power(i))
+            if i % 2 == 1:
+                v_work.setdefault(un + HL, []).insert(0, lambda i=i: h_quant(i // 2))
+        v_work.setdefault(1, []).append(lambda: r_quant(*r_parts[6]))
+        if R7E == "v":
+            v_work.setdefault(R7, []).insert(0, lambda: r_group(*r_parts[7], "v"))
+        else:
+            s_work.setdefault(R7, []).insert(0, lambda: r_group(*r_parts[7], "s"))
+        v_work.setdefault(R7 + 1, []).append(lambda: r_quant(*r_parts[7]))
+        h_turn_at.setdefault(0, []).insert(0, 2)
+        h_mul(3)
+        for un in range(nu + 1):
+            if un + 1 < nu:
                 for t in range(4):
-                    product(un, t)
-            if un >= 2:
-                y_quant(un - 2)
-            if 1 <= un <= nu:
-                if CAST[un - 1] == "sv":
-                    y_round(un - 1, "v", 0, 2)
-                    y_round(un - 1, "s", 1, 2)
-                else:
-                    y_round(un - 1, CAST[un - 1])
-            for f in s_work.get(un, []) + v_work.get(un, []):
+                    product(un + 1, t)
+            if un >= 1 and GCOLS[un - 1] > 0:
+                y_round(un - 1, "g", 0, GCOLS[un - 1])
+            if 1 <= un <= nu - VLAST and GCOLS[un - 1] < UNITS[un - 1][1]:
+                y_round(un - 1, "s", GCOLS[un - 1], UNITS[un - 1][1])
+            for f in s_work.get(un, []):
                 f()
             if un < nu:
                 for t in range(4):
                     times_schedule(un, t)
-            if 1 <= un <= nu:
+            if un >= 1:
                 for k in range(UNITS[un - 1][1] // P):
-                    turn_back(un - 1, k)
-            if 1 <= un <= 4:
-                h_turn(un + 3, "s")
-            if un + 3 < nu:
-                s_turn_unit(un + 3, "s")
-        store_scales()
+                    turn_back(un - 1, k, "v" if (un == nu or (k == 0 and un in VCOPY)) else "s")
+            for i in h_turn_at.get(un, []):
+                h_turn(i, "s")
+            for args in s_left[SG + sum(SL[:un]) : SG + sum(SL[: un + 1])]:
+                s_turn(*args, "s")
+            if un > nu - VLAST:
+                y_round(un - 1, "v", 0, UNITS[un - 1][1])
+            for f in v_work.get(un, []):
+                f()
+            if un >= 1:
+                y_quant(un - 1)
+            if un - 1 == 7:
+                store_scales(0, W)
+        store_scales(W, M)

@@ -18,23 +18,14 @@ ALU = mybir.AluOpType
 
 P = 128
 W = 512
+ROWS = 256
 LN_FLOOR = 2.0 ** -60
-R0 = 2
-NR = 6
-YB = 1
-SG = 2
-HL = 2
-VCOPY = ()
-R7E = "v"
-R7 = 0
-HM = ((3, -1), (4, 2), (5, 3), (6, 5), (7, 7))
-SL = (1,) * 8
-GCOLS = [176] * 15 + [64, 0]
-VLAST = 1
-ROT = (0, 1, 13, 2, 3, 14)
-UNITS = [(0, 256, q) for q in range(3)] + [(256, 256, q) for q in range(3)] + [(0, 256, 3), (256, 256, 3)] + [(256 * r, 256, q) for r in (2, 3) for q in range(4)][:-1] + [(768, 128, 3), (896, 128, 3)]
 X_CHUNKS = ((0, 256), (256, 512), (512, 1024))
-
+UNITS = [(ROWS * r, ROWS, q) for r in range(4) for q in range(4)][:-1] + [(768, P, 3), (896, P, 3)]
+GPSIMD_SLOTS = 2
+GPSIMD_SHARE = 9
+HEAD_PASSES = (12, 8, 2)
+LONG_WAIT_PASSES = 6
 
 def tile_cube_root_impact_cost_h2_kernel(
     tc, flow_words, flow_scales, impact_words, impact_scales, depth_gain, response, drift, schedule,
@@ -43,23 +34,38 @@ def tile_cube_root_impact_cost_h2_kernel(
     nc = tc.nc
     with ExitStack() as ctx:
         keep = ctx.enter_context(tc.tile_pool(name="keep", bufs=1))
-        flow = ctx.enter_context(tc.tile_pool(name="flow", bufs=2))
+        ring = ctx.enter_context(tc.tile_pool(name="ring", bufs=2))
         psum = ctx.enter_context(tc.psum_pool(name="psum", bufs=1))
         ctx.enter_context(tc.manual_schedule())
 
+        free_banks = list(range(8))
         banks_taken = []
 
-        def bank():
-            n = len(banks_taken)
-            tile = psum.tile([P, W], F32, name="bank%d" % n, tag="bank%d" % (n % 8))
-            banks_taken.append(tile)
+        def take_bank():
+            number = free_banks.pop(0)
+            tile = psum.tile([P, W], F32, name="bank%d" % len(banks_taken), tag="bank%d" % number)
+            banks_taken.append((tile, number))
             return tile
 
-        def big(shape, dtype, slot, name):
-            return keep.tile(shape, dtype, name=name, tag="big%d" % slot, align_bytes=64)
+        def give_back(tile):
+            free_banks.append([number for taken, number in banks_taken if taken is tile][0])
 
-        def small(shape, dtype, slot, name):
-            return keep.tile(shape, dtype, name=name, tag="small%d" % slot, align_bytes=64)
+        def big(shape, dtype, place, name):
+            return keep.tile(shape, dtype, name=name, tag="big%d" % place, align_bytes=64)
+
+        def small(shape, dtype, place, name):
+            return keep.tile(shape, dtype, name=name, tag="small%d" % place, align_bytes=64)
+
+        def staging(shape, place, name):
+            return keep.tile(shape, BF16, name=name, tag="staging%d" % place, align_bytes=64)
+
+        def copy_on(engine, dst, src):
+            if engine == "scalar":
+                nc.scalar.copy(out=dst, in_=src)
+            elif engine == "gpsimd":
+                nc.gpsimd.tensor_scalar(out=dst, in0=src, scalar1=1.0, scalar2=0.0, op0=ALU.mult, op1=ALU.add)
+            else:
+                nc.vector.tensor_copy(out=dst, in_=src)
 
         x_scales = []
         g_scales = []
@@ -68,105 +74,107 @@ def tile_cube_root_impact_cost_h2_kernel(
                 plane = keep.tile([P, 4, W], U8, name=name % half, align_bytes=64)
                 nc.vector.memset(plane[:].bitcast(I32), 0)
                 planes.append(plane)
-        gain_pairs = keep.tile([P, 2, 4], BF16, name="gain_pairs")
-        nc.gpsimd.dma_start(out=gain_pairs[:], in_=depth_gain.rearrange("(g p t) -> p g t", g=2, t=4))
+        gain_words = keep.tile([P, 2, 4], BF16, name="gain_words")
+        nc.gpsimd.dma_start(out=gain_words[:], in_=depth_gain.rearrange("(g p t) -> p g t", g=2, t=4))
         ident = keep.tile([P, P], F32, name="ident")
         make_identity(nc, ident[:])
-        warm = keep.tile([P, 1], F32, name="warm")
-        nc.scalar.activation(out=warm[:], in_=ident[:, 0:1], func=ACT.Ln, bias=1.0)
+        zero = keep.tile([P, 1], F32, name="zero")
+        nc.scalar.activation(out=zero[:], in_=ident[:, 0:1], func=ACT.Ln, scale=0.0, bias=1.0)
 
+        ones = keep.tile([P, W], BF16, name="ones", align_bytes=64)
+        ones_codes = keep.tile([P, P], U32, name="ones_codes", align_bytes=64)
+        ones_scales = keep.tile([P, P], U8, name="ones_scales", align_bytes=64)
+        nc.vector.memset(ones[:], 1.0)
+        nc.vector.quantize_mx(out=ones_codes[:].bitcast(FP8X4), scales=ones_scales[:], in_=ones[:])
+
+        def warm_up(bank, passes, rhs, rhs_scale, columns):
+            for repeat in range(passes):
+                nc.tensor.matmul_mx(
+                    out=bank[:, 0:columns], lhsT=ones_codes[:].bitcast(FP8X4), lhsT_scale=ones_scales[:],
+                    rhs=rhs, rhs_scale=rhs_scale, start=True, stop=True,
+                )
         g_words = []
         x_words = []
+        r_raw = {}
+        s_raw = {}
 
         def load_g(half):
             tile = small([P, 4, 2 * W], U8, half, "g_words%d" % half)
-            nc.sync.dma_start(
-                out=tile[:].bitcast(I32),
-                in_=impact_words[:, :, 2 * W * half : 2 * W * (half + 1)].rearrange("g p b -> p g b").bitcast(I32),
-            )
+            cols = impact_words[:, :, 2 * W * half : 2 * W * (half + 1)]
+            nc.sync.dma_start(out=tile[:].bitcast(I32), in_=cols.rearrange("g p b -> p g b").bitcast(I32))
             g_words.append(tile)
 
-        def load_x(c):
-            m0, m1 = X_CHUNKS[c]
+        def load_x(chunk):
+            m0, m1 = X_CHUNKS[chunk]
             if m1 - m0 == W:
-                tile = big([P, 4, W], U32, 8, "x_words%d" % c)
+                tile = big([P, 4, W], U32, 8, "x_words%d" % chunk)
             else:
-                tile = small([P, 4, m1 - m0], U32, 2 + c, "x_words%d" % c)
-            nc.sync.dma_start(
-                out=tile[:].bitcast(I32),
-                in_=flow_words[:, :, m0:m1, :].rearrange("g p m t -> p g (m t)").bitcast(I32),
-            )
+                tile = small([P, 4, m1 - m0], U32, 2 + chunk, "x_words%d" % chunk)
+            cols = flow_words[:, :, m0:m1, :]
+            nc.sync.dma_start(out=tile[:].bitcast(I32), in_=cols.rearrange("g p m t -> p g (m t)").bitcast(I32))
             x_words.append(tile)
 
-        def load_scales(planes, scales, half, on_sync=4):
-            for quad in range(4):
-                queue = nc.sync if quad < on_sync else nc.gpsimd
+        def load_scales(planes, scales, half, queues):
+            for quad, queue in enumerate(queues):
                 rows = scales[:, 4 * quad : 4 * quad + 4, W * half : W * (half + 1)]
                 queue.dma_start(
                     out=planes[half][32 * quad : 32 * quad + 4, :, :].bitcast(I32),
                     in_=rows.rearrange("g r n -> r g n").bitcast(I32),
                 )
 
-        r_raw = {}
+        def load_r(g, half):
+            r_raw[g, half] = big([P, 4, 2 * W], BF16, 9 + 2 * half + g, "r_raw%d%d" % (g, half))
+            rows = response[W * g : W * (g + 1), 2 * W * half : 2 * W * (half + 1)]
+            nc.sync.dma_start(out=r_raw[g, half][:], in_=rows.rearrange("(p j) n -> p j n", j=4))
 
-        def load_r(g, nh):
-            tile = big([P, 4, 2 * W], BF16, 9 + 2 * nh + g, "r_raw%d%d" % (g, nh))
-            nc.sync.dma_start(
-                out=tile[:],
-                in_=response[W * g : W * (g + 1), 2 * W * nh : 2 * W * (nh + 1)].rearrange("(p j) n -> p j n", j=4),
-            )
-            r_raw[g, nh] = tile
+        def load_s(r, place):
+            s_raw[r] = big([P, 2, N], BF16, place, "s_raw%d" % r)
+            rows = schedule[ROWS * r : ROWS * (r + 1), :]
+            nc.sync.dma_start(out=s_raw[r][:], in_=rows.rearrange("(i p) n -> p i n", p=P))
 
-        s_tiles = {}
-
-        def load_s(h, nh, slot):
-            tile = big([P, 4, 2 * W], BF16, slot, "s%d%d" % (h, nh))
-            nc.sync.dma_start(
-                out=tile[:],
-                in_=schedule[W * h : W * (h + 1), 2 * W * nh : 2 * W * (nh + 1)].rearrange("(i p) n -> p i n", p=P),
-            )
-            s_tiles[h, nh] = tile
-
-        drift_col = keep.tile([P, 4, 4], BF16, name="drift_col")
+        drift_words = keep.tile([P, 4, 4], BF16, name="drift_words")
         load_g(0)
         load_x(0)
-        load_scales(g_scales, impact_scales, 0)
-        load_scales(x_scales, flow_scales, 0, 2)
+        load_scales(g_scales, impact_scales, 0, [nc.sync] * 4)
+        load_scales(x_scales, flow_scales, 0, [nc.sync] * 2 + [nc.gpsimd] * 2)
         load_x(1)
         load_g(1)
-        load_scales(g_scales, impact_scales, 1)
+        load_scales(g_scales, impact_scales, 1, [nc.sync] * 4)
         load_r(0, 0)
         load_x(2)
-        load_scales(x_scales, flow_scales, 1)
+        load_scales(x_scales, flow_scales, 1, [nc.sync] * 4)
         load_r(1, 0)
         load_r(0, 1)
-        load_s(0, 0, 13)
+        load_s(0, 13)
         load_r(1, 1)
-        load_s(0, 1, 14)
-        nc.sync.dma_start(out=drift_col[:], in_=drift.rearrange("(g p t) -> p g t", g=4, t=4))
-        load_s(1, 0, 15)
+        load_s(1, 14)
+        nc.sync.dma_start(out=drift_words[:], in_=drift.rearrange("(q p t) -> p q t", q=4, t=4))
+        load_s(2, 15)
 
         gain_all = keep.tile([P, A], BF16, name="gain_all")
 
         def spread_gain():
-            gb = bank()
-            gain_w = gain_pairs[:].rearrange("p g t -> p (g t)").bitcast(F32)
+            bank = take_bank()
+            pairs = gain_words[:].rearrange("p g t -> p (g t)").bitcast(F32)
             for c in range(4):
-                nc.tensor.transpose(gb[:, P * c : P * (c + 1)], gain_w[:, c : c + 1].to_broadcast([P, P]), ident[:])
-            nc.vector.tensor_copy(out=gain_all[:].bitcast(F32), in_=gb[:])
+                nc.tensor.transpose(bank[:, P * c : P * (c + 1)], pairs[:, c : c + 1].to_broadcast([P, P]), ident[:])
+            nc.vector.tensor_copy(out=gain_all[:].bitcast(F32), in_=bank[:])
+            give_back(bank)
 
-        mag = {}
-        ug = {}
-        u_banks = {}
+        power = {}
+        u_gain = {}
 
-        def stage1(i, g):
-            c = [n for n, (m0, m1) in enumerate(X_CHUNKS) if m0 <= P * i < m1][0]
-            col = P * i - X_CHUNKS[c][0]
-            u = bank()
+        def by_pairs(cols):
+            return cols.rearrange("m (u p e) -> m u p e", u=2, e=2)
+
+        def pressure(i, g):
+            chunk = [n for n, (m0, m1) in enumerate(X_CHUNKS) if m0 <= P * i < m1][0]
+            col = P * i - X_CHUNKS[chunk][0]
+            bank = take_bank()
             for k in range(4):
                 nc.tensor.matmul_mx(
-                    out=u[:],
-                    lhsT=x_words[c][:, k, col : col + P].bitcast(FP8X4),
+                    out=bank[:],
+                    lhsT=x_words[chunk][:, k, col : col + P].bitcast(FP8X4),
                     lhsT_scale=x_scales[i // 4][:, k, P * (i % 4) : P * (i % 4 + 1)],
                     rhs=g_words[g][:, k, :].bitcast(FP4X4),
                     rhs_scale=g_scales[g][:, k, :],
@@ -174,199 +182,195 @@ def tile_cube_root_impact_cost_h2_kernel(
                     stop=(k == 3),
                 )
             if g == 0:
-                both = big([P, 2, A], F32, i, "mag_ug%d" % i)
-                mag[i] = both[:, 0, :]
-                ug[i] = both[:, 1, :]
-            u_sorted = u[:].rearrange("m (p u e) -> m u p e", u=2, e=2)
+                both = big([P, 2, A], F32, i, "power_and_u_gain%d" % i)
+                power[i] = both[:, 0, :]
+                u_gain[i] = both[:, 1, :]
+            u_sorted = bank[:].rearrange("m (p u e) -> m u p e", u=2, e=2)
             cols = slice(W * g, W * (g + 1))
-            nc.scalar.activation(
-                out=mag[i][:, cols].rearrange("m (u p e) -> m u p e", u=2, e=2), in_=u_sorted, func=ACT.Abs
-            )
-            u_banks[i, g] = u_sorted
-
-        def times_gain(i, g):
-            cols = slice(W * g, W * (g + 1))
-            u_sorted = u_banks[i, g]
+            nc.scalar.activation(out=by_pairs(power[i][:, cols]), in_=u_sorted, func=ACT.Abs, bias=zero[:])
             nc.vector.tensor_tensor(
-                out=ug[i][:, cols].rearrange("m (u p e) -> m u p e", u=2, e=2),
-                in0=u_sorted,
-                in1=gain_all[:, cols].rearrange("m (u p e) -> m u p e", u=2, e=2),
-                op=ALU.mult,
+                out=by_pairs(u_gain[i][:, cols]), in0=u_sorted, in1=by_pairs(gain_all[:, cols]), op=ALU.mult
             )
+            give_back(bank)
 
-        def log_mag(i, g):
-            part = mag[i][:, W * g : W * (g + 1)]
+        def take_log(i, g):
+            part = power[i][:, W * g : W * (g + 1)]
             nc.scalar.activation(out=part, in_=part, func=ACT.Ln, bias=LN_FLOOR)
 
-        def power(i):
-            nc.scalar.activation(out=mag[i][:], in_=mag[i][:], func=ACT.Exp, scale=-2.0 / 3.0)
+        def take_exp(i):
+            nc.scalar.activation(out=power[i], in_=power[i], func=ACT.Exp, scale=-2.0 / 3.0)
 
         h_bf = {}
+        h_banks = {}
         h_t = {}
         h_codes = keep.tile([P, 2, M], U32, name="h_codes", align_bytes=64)
         h_scales = keep.tile([P, 2, M], U8, name="h_scales", align_bytes=64)
 
-        def copy_on(eng, dst, src):
-            if eng == "s":
-                nc.scalar.copy(out=dst, in_=src)
-            elif eng == "g":
-                nc.gpsimd.tensor_scalar(out=dst, in0=src, scalar1=1.0, scalar2=0.0, op0=ALU.mult, op1=ALU.add)
-            else:
-                nc.vector.tensor_copy(out=dst, in_=src)
+        def h_multiply(i):
+            h_bf[i] = ring.tile([P, A], BF16, name="h_bf%d" % i, tag="h_bf")
+            nc.vector.tensor_tensor(out=h_bf[i][:], in0=u_gain[i], in1=power[i], op=ALU.mult)
 
-        def h_mul(i):
-            h_bf[i] = flow.tile([P, A], BF16, name="h_bf%d" % i, tag="h_bf")
-            nc.vector.tensor_tensor(out=h_bf[i][:], in0=ug[i][:], in1=mag[i][:], op=ALU.mult)
-
-        def h_turn(i, eng):
-            pair, r = divmod(i, 2)
-            if r == 0:
-                h_t[pair] = flow.tile([P, 2, 2 * P, 4], BF16, name="h_t%d" % pair, tag="h_t", align_bytes=64)
-            b = bank()
-            words = h_bf[i][:].bitcast(F32)
+        def h_transpose(i):
+            h_banks[i] = take_bank()
+            pairs = h_bf[i][:].bitcast(F32)
             for c in range(4):
-                nc.tensor.transpose(b[:, P * c : P * (c + 1)], words[:, P * c : P * (c + 1)], ident[:])
-            dst = h_t[pair][:].bitcast(F32)[:, :, P * r : P * (r + 1), :]
-            copy_on(eng, dst, b[:].rearrange("p (g u m) -> p g m u", g=2, u=2))
+                nc.tensor.transpose(h_banks[i][:, P * c : P * (c + 1)], pairs[:, P * c : P * (c + 1)], ident[:])
 
-        def h_quant(pair):
+        def h_copy_out(i):
+            r, which = divmod(i, 2)
+            if which == 0:
+                h_t[r] = staging([P, 2, ROWS, 4], 2 + r % 2, "h_t%d" % r)
+            dst = h_t[r][:].bitcast(F32)[:, :, P * which : P * (which + 1), :]
+            nc.scalar.copy(out=dst, in_=h_banks[i][:].rearrange("p (g u m) -> p g m u", u=2, m=P))
+            give_back(h_banks[i])
+
+        def h_quantize(r):
             for g in range(2):
                 nc.vector.quantize_mx(
-                    out=h_codes[:, g, 2 * P * pair : 2 * P * (pair + 1)].bitcast(FP8X4),
-                    scales=h_scales[:, g, 2 * P * pair : 2 * P * (pair + 1)],
-                    in_=h_t[pair][:, g, :, :].rearrange("p m t -> p (m t)"),
+                    out=h_codes[:, g, ROWS * r : ROWS * (r + 1)].bitcast(FP8X4),
+                    scales=h_scales[:, g, ROWS * r : ROWS * (r + 1)],
+                    in_=h_t[r][:, g, :, :].rearrange("p m t -> p (m t)"),
                 )
 
         r_codes = keep.tile([P, 2, N], U32, name="r_codes", align_bytes=64)
         r_scales = keep.tile([P, 2, N], U8, name="r_scales", align_bytes=64)
-        r_grouped = {}
+        r_laid = {}
 
-        def r_group(g, q, eng="v"):
-            t = flow.tile([P, W, 4], BF16, name="r_grp%d%d" % (g, q), tag="r_grp", bufs=3, align_bytes=64)
+        def r_lay_out(part, engine, t0, t1):
+            g, q = part
+            if part not in r_laid:
+                r_laid[part] = staging([P, W, 4], len(r_laid) % 2, "r_laid%d%d" % part)
             src = r_raw[g, q // 2][:, :, W * (q % 2) : W * (q % 2 + 1)].rearrange("p j (c m t) -> p t c j m", m=2, t=4)
-            dst = t[:].rearrange("p (t c m) j -> p t c j m", t=4, m=2)
-            copy_on(eng, dst, src)
-            r_grouped[g, q] = t
+            dst = r_laid[part][:].rearrange("p (t c m) j -> p t c j m", t=4, m=2)
+            if engine == "gpsimd":
+                for t in range(t0, t1):
+                    copy_on(engine, dst[:, t], src[:, t])
+            else:
+                copy_on(engine, dst[:, t0:t1], src[:, t0:t1])
 
-        def r_quant(g, q):
+        def r_quantize(part):
+            g, q = part
             nc.vector.quantize_mx(
                 out=r_codes[:, g, W * q : W * (q + 1)].bitcast(FP8X4),
                 scales=r_scales[:, g, W * q : W * (q + 1)],
-                in_=r_grouped[g, q][:].rearrange("p n t -> p (n t)"),
+                in_=r_laid[part][:].rearrange("p n j -> p (n j)"),
             )
-
-        s_t = {}
-        y_t = {}
-        y_bf = {}
-        y = {}
-        y_scales = keep.tile([P, M], U8, name="y_scales", align_bytes=64)
-        slots_taken = []
-
-        def next_big(shape, name):
-            n = len(slots_taken)
-            slots_taken.append(n)
-            return big(shape, F32, ROT[n % len(ROT)], name)
 
         s_banks = {}
-        s_part = {}
+        s_tiles = {}
+        s_t = {}
 
-        def s_keep(h, q, part, eng):
-            if h == 0:
-                if part == 0:
-                    s_t[h, q] = small([P, 2, W], F32, q, "s_t%d%d" % (h, q))
-                dst = s_t[h, q][:, :, 2 * P * part : 2 * P * (part + 1)]
-            else:
-                if q == 0:
-                    s_t[h, part] = big([P, 4, 2, 2 * P], F32, 9 + part, "s_t%d%d" % (h, part))
-                dst = s_t[h, part][:, q, :, :]
-            s_part[2 * h + part, q] = dst
-            b = s_banks[h, q, part]
-            copy_on(eng, dst, b[:].rearrange("p (u m) -> p u m", u=2))
-
-        def s_flip(h, q, part):
-            b = bank()
-            s_banks[h, q, part] = b
+        def s_transpose(r, q):
+            s_banks[r, q] = take_bank()
             for u in range(2):
                 for c in range(2):
-                    words = s_tiles[h, q // 2][:, 2 * part + c, W * (q % 2) : W * (q % 2 + 1)].bitcast(F32)
-                    nc.tensor.transpose(b[:, P * (2 * u + c) : P * (2 * u + c + 1)], words[:, u : 2 * P : 2], ident[:])
+                    pairs = s_raw[r][:, c, W * q : W * (q + 1)].bitcast(F32)
+                    out = s_banks[r, q][:, P * (2 * u + c) : P * (2 * u + c + 1)]
+                    nc.tensor.transpose(out, pairs[:, u : 2 * P : 2], ident[:])
 
-        def s_turn(h, q, part, eng):
-            s_flip(h, q, part)
-            s_keep(h, q, part, eng)
+        def s_copy_out(r, q, engine):
+            if r < 2:
+                if r == 0:
+                    s_tiles["small", q] = small([P, 2, 2 * ROWS], F32, (q + 2) % 4, "s_t_small%d" % q)
+                s_t[r, q] = s_tiles["small", q][:, :, ROWS * r : ROWS * (r + 1)]
+            else:
+                if q == 0:
+                    s_tiles["big", r] = big([P, 4, 2, ROWS], F32, 7 + r, "s_t_big%d" % r)
+                s_t[r, q] = s_tiles["big", r][:, q, :, :]
+            copy_on(engine, s_t[r, q], s_banks[r, q][:].rearrange("p (u m) -> p u m", u=2))
+            give_back(s_banks[r, q])
 
         d_banks = {}
+        y_t = {}
+        y_banks = {}
+        y = {}
+        y_bf = {}
+        y_scales = keep.tile([P, M], U8, name="y_scales", align_bytes=64)
+        y_places = (0, 1, 13, 14, 2, 3)
+        y_tiles_made = []
 
-        def product(un, t):
-            m0, mw, q = UNITS[un]
-            per_bank = W // mw
-            if t % per_bank == 0:
-                d_banks[un, t // per_bank] = bank()
-            n0 = W * q + P * t
-            for g in range(2):
-                nc.tensor.matmul_mx(
-                    out=d_banks[un, t // per_bank][:, mw * (t % per_bank) : mw * (t % per_bank + 1)],
-                    lhsT=r_codes[:, g, n0 : n0 + P].bitcast(FP8X4),
-                    lhsT_scale=r_scales[:, g, n0 : n0 + P],
-                    rhs=h_codes[:, g, m0 : m0 + mw].bitcast(FP8X4),
-                    rhs_scale=h_scales[:, g, m0 : m0 + mw],
-                    start=(g == 0),
-                    stop=(g == 1),
-                )
+        def y_tile(shape, name):
+            y_tiles_made.append(name)
+            return big(shape, F32, y_places[(len(y_tiles_made) - 1) % len(y_places)], name)
 
-        def times_schedule(un, t):
-            m0, mw, q = UNITS[un]
-            per_bank = W // mw
-            if t == 0:
-                y_t[un] = next_big([P, 4, mw], "y_t%d" % un)
-            u, e = divmod(t, 2)
-            nc.vector.scalar_tensor_tensor(
-                out=y_t[un][:, t, :],
-                in0=d_banks[un, t // per_bank][:, mw * (t % per_bank) : mw * (t % per_bank + 1)],
-                scalar=drift_col[:, q, t : t + 1],
-                in1=s_part[m0 // (2 * P), q][:, u, m0 % (2 * P) : m0 % (2 * P) + mw].bitcast(BF16)[:, e : 2 * mw : 2],
-                op0=ALU.add,
-                op1=ALU.mult,
-            )
+        def d_slot(unit, t):
+            width = UNITS[unit][1]
+            index, within = divmod(t, W // width)
+            return d_banks[unit][index][:, width * within : width * (within + 1)]
 
-        def turn_back(un, i, eng="s"):
-            m0, mw, q = UNITS[un]
-            b = bank()
+        def price_move(unit):
+            m0, width, q = UNITS[unit]
+            d_banks[unit] = []
             for t in range(4):
-                nc.tensor.transpose(b[:, P * t : P * (t + 1)], y_t[un][:, t, P * i : P * (i + 1)], ident[:])
-            if i == 0:
-                y[un] = next_big([P, mw // P, W], "y%d" % un)
-            copy_on(eng, y[un][:, i, :].rearrange("m (p t) -> m p t", t=4), b[:].rearrange("m (t p) -> m p t", t=4))
-            per_store = min(2, mw // P)
-            if i % per_store == per_store - 1:
-                i0 = i - per_store + 1
-                nc.sync.dma_start(
-                    out=out_0[m0 + P * i0 : m0 + P * (i + 1), W * q : W * (q + 1)].rearrange("(i p) n -> p i n", p=P),
-                    in_=y[un][:, i0 : i + 1, :],
-                )
+                if t % (W // width) == 0:
+                    d_banks[unit].append(take_bank())
+                n0 = W * q + P * t
+                for g in range(2):
+                    nc.tensor.matmul_mx(
+                        out=d_slot(unit, t),
+                        lhsT=r_codes[:, g, n0 : n0 + P].bitcast(FP8X4),
+                        lhsT_scale=r_scales[:, g, n0 : n0 + P],
+                        rhs=h_codes[:, g, m0 : m0 + width].bitcast(FP8X4),
+                        rhs_scale=h_scales[:, g, m0 : m0 + width],
+                        start=(g == 0),
+                        stop=(g == 1),
+                    )
 
-        def y_round(un, eng, c0, c1):
-            m0, mw, q = UNITS[un]
-            if un not in y_bf:
-                y_bf[un] = flow.tile([P, mw, 4], BF16, name="y_bf%d" % un, tag="y_bf", bufs=YB, align_bytes=64)
+        def cost(unit):
+            m0, width, q = UNITS[unit]
+            r, first = divmod(m0, ROWS)
+            y_t[unit] = y_tile([P, 4, width], "y_t%d" % unit)
+            for t in range(4):
+                u, e = divmod(t, 2)
+                nc.vector.scalar_tensor_tensor(
+                    out=y_t[unit][:, t, :],
+                    in0=d_slot(unit, t),
+                    scalar=drift_words[:, q, t : t + 1],
+                    in1=s_t[r, q][:, u, first : first + width].bitcast(BF16)[:, e : 2 * width : 2],
+                    op0=ALU.add,
+                    op1=ALU.mult,
+                )
+            for bank in d_banks[unit]:
+                give_back(bank)
+
+        def y_transpose(unit):
+            y_banks[unit] = []
+            for i in range(UNITS[unit][1] // P):
+                bank = take_bank()
+                y_banks[unit].append(bank)
+                for t in range(4):
+                    nc.tensor.transpose(bank[:, P * t : P * (t + 1)], y_t[unit][:, t, P * i : P * (i + 1)], ident[:])
+
+        def y_copy_out_and_store(unit, last_engine):
+            m0, width, q = UNITS[unit]
+            y[unit] = y_tile([P, width // P, W], "y%d" % unit)
+            for i, bank in enumerate(y_banks[unit]):
+                engine = last_engine if i == width // P - 1 else "scalar"
+                dst = y[unit][:, i, :].rearrange("m (p t) -> m p t", t=4)
+                copy_on(engine, dst, bank[:].rearrange("m (t p) -> m p t", t=4))
+                give_back(bank)
+            rows = out_0[m0 : m0 + width, W * q : W * (q + 1)]
+            nc.sync.dma_start(out=rows.rearrange("(i p) n -> p i n", p=P), in_=y[unit][:])
+
+        def y_round(unit, engine, c0, c1):
+            if unit not in y_bf:
+                y_bf[unit] = keep.tile([P, UNITS[unit][1], 4], BF16, name="y_bf%d" % unit, tag="y_bf", align_bytes=64)
             copy_on(
-                eng,
-                y_bf[un][:, c0:c1, :].rearrange("p (c i) t -> p c t i", i=4),
-                y_t[un][:, :, c0:c1].rearrange("p t (c i) -> p c t i", i=4),
+                engine,
+                y_bf[unit][:, c0:c1, :].rearrange("p (c i) t -> p c t i", i=4),
+                y_t[unit][:, :, c0:c1].rearrange("p t (c i) -> p c t i", i=4),
             )
 
-        def y_quant(un):
-            m0, mw, q = UNITS[un]
-            codes = flow.tile([P, mw], U32, name="y_codes%d" % un, tag="y_codes", bufs=4, align_bytes=64)
+        def y_quantize_and_store(unit):
+            m0, width, q = UNITS[unit]
+            codes = ring.tile([P, width], U32, name="y_codes%d" % unit, tag="y_codes", bufs=4, align_bytes=64)
             nc.vector.quantize_mx(
                 out=codes[:].bitcast(FP8X4),
-                scales=y_scales[4 * q : P, m0 : m0 + mw],
-                in_=y_bf[un][:].rearrange("p m t -> p (m t)"),
+                scales=y_scales[4 * q : P, m0 : m0 + width],
+                in_=y_bf[unit][:].rearrange("p m t -> p (m t)"),
             )
-            nc.sync.dma_start(
-                out=out_1[q, :, m0 : m0 + mw, :].rearrange("p m t -> p (m t)").bitcast(I32),
-                in_=codes[:].bitcast(I32),
-            )
+            words = out_1[q, :, m0 : m0 + width, :].rearrange("p m t -> p (m t)")
+            nc.sync.dma_start(out=words.bitcast(I32), in_=codes[:].bitcast(I32))
 
         def store_scales(m0, m1):
             for quad in range(4):
@@ -377,89 +381,109 @@ def tile_cube_root_impact_cost_h2_kernel(
 
         r_parts = [(0, 0), (0, 1), (1, 0), (1, 1), (0, 2), (1, 2), (0, 3), (1, 3)]
         order = [(i, g) for g in range(2) for i in range(4)] + [(i, g) for i in range(4, 8) for g in range(2)]
+        unread = take_bank()
+        warm_up(unread, HEAD_PASSES[0], ones_codes[:].bitcast(FP8X4), ones_scales[:], P)
         spread_gain()
+        warm_up(unread, HEAD_PASSES[1], x_words[0][:, 0, 0:P].bitcast(FP8X4), ones_scales[:], P)
+        warm_up(unread, HEAD_PASSES[2], g_words[0][:, 0, :].bitcast(FP4X4), g_scales[0][:, 0, :], W)
+        give_back(unread)
         for n, (i, g) in enumerate(order):
-            stage1(i, g)
-            times_gain(i, g)
+            turn, position = divmod(n, 4)
+            last_turn = turn == 3
+            if position == 0 and turn > 0:
+                r_lay_out(r_parts[2 * turn - 1], "gpsimd", 0, 4 if last_turn else GPSIMD_SLOTS)
+            pressure(i, g)
             if n >= 1:
-                log_mag(*order[n - 1])
-            if n >= R0 and (n - R0) % 2 == 0 and (n - R0) // 2 < NR:
-                r_group(*r_parts[(n - R0) // 2])
-            if n >= R0 and (n - R0) % 2 == 1 and (n - R0) // 2 < NR:
-                r_quant(*r_parts[(n - R0) // 2])
-        log_mag(*order[-1])
-        load_s(1, 1, 8)
-        early = [(0, q, part) for part in range(2) for q in range(3)]
-        s_left = [(0, 3, 0), (0, 3, 1)] + [(1, q, part) for part in range(2) for q in range(4)]
-        for args in early:
-            s_flip(*args)
-        s_keep(*early[0], "v")
-        s_keep(*early[1], "v")
-        power(0)
-        power(1)
-        h_mul(0)
-        s_keep(*early[2], "s")
-        s_keep(*early[3], "s")
-        h_mul(1)
-        h_turn(0, "v")
-        power(2)
-        h_turn(1, "v")
-        s_keep(*early[4], "s")
-        s_keep(*early[5], "s")
-        power(3)
-        h_mul(2)
-        h_quant(0)
-        for args in s_left[:SG]:
-            s_turn(*args, "s")
-        for t in range(4):
-            product(0, t)
-        power(4)
-        r_group(*r_parts[6], "s")
-        nu = len(UNITS)
-        v_work = {}
-        s_work = {}
-        h_turn_at = {}
-        for i, un in HM:
-            v_work.setdefault(un, []).append(lambda i=i: h_mul(i))
-            h_turn_at.setdefault(un + 1, []).append(i)
-            if i > 4:
-                s_work.setdefault(un - 1, []).append(lambda i=i: power(i))
-            if i % 2 == 1:
-                v_work.setdefault(un + HL, []).insert(0, lambda i=i: h_quant(i // 2))
-        v_work.setdefault(1, []).append(lambda: r_quant(*r_parts[6]))
-        if R7E == "v":
-            v_work.setdefault(R7, []).insert(0, lambda: r_group(*r_parts[7], "v"))
-        else:
-            s_work.setdefault(R7, []).insert(0, lambda: r_group(*r_parts[7], "s"))
-        v_work.setdefault(R7 + 1, []).append(lambda: r_quant(*r_parts[7]))
-        h_turn_at.setdefault(0, []).insert(0, 2)
-        h_mul(3)
-        for un in range(nu + 1):
-            if un + 1 < nu:
-                for t in range(4):
-                    product(un + 1, t)
-            if un >= 1 and GCOLS[un - 1] > 0:
-                y_round(un - 1, "g", 0, GCOLS[un - 1])
-            if 1 <= un <= nu - VLAST and GCOLS[un - 1] < UNITS[un - 1][1]:
-                y_round(un - 1, "s", GCOLS[un - 1], UNITS[un - 1][1])
-            for f in s_work.get(un, []):
-                f()
-            if un < nu:
-                for t in range(4):
-                    times_schedule(un, t)
-            if un >= 1:
-                for k in range(UNITS[un - 1][1] // P):
-                    turn_back(un - 1, k, "v" if (un == nu or (k == 0 and un in VCOPY)) else "s")
-            for i in h_turn_at.get(un, []):
-                h_turn(i, "s")
-            for args in s_left[SG + sum(SL[:un]) : SG + sum(SL[: un + 1])]:
-                s_turn(*args, "s")
-            if un > nu - VLAST:
-                y_round(un - 1, "v", 0, UNITS[un - 1][1])
-            for f in v_work.get(un, []):
-                f()
-            if un >= 1:
-                y_quant(un - 1)
-            if un - 1 == 7:
-                store_scales(0, W)
-        store_scales(W, M)
+                take_log(*order[n - 1])
+            if position == 3 and not last_turn:
+                r_lay_out(r_parts[2 * turn], "vector", 0, 4)
+                if turn > 0:
+                    r_lay_out(r_parts[2 * turn - 1], "vector", GPSIMD_SLOTS, 4)
+                r_quantize(r_parts[2 * turn])
+                if turn > 0:
+                    r_quantize(r_parts[2 * turn - 1])
+        take_log(*order[-1])
+        load_s(3, 8)
+
+        unread = take_bank()
+
+        def stay_warm(passes=2):
+            warm_up(unread, passes, r_codes[:, 0, 0:W].bitcast(FP8X4), r_scales[:, 0, 0:W], W)
+
+        for q in range(4):
+            s_transpose(0, q)
+            s_copy_out(0, q, "vector")
+            if q % 2 == 1:
+                stay_warm(LONG_WAIT_PASSES if q == 1 else 2)
+        for q in range(4):
+            s_transpose(1, q)
+            if q % 2 == 1:
+                stay_warm()
+        take_exp(0)
+        take_exp(1)
+        h_multiply(0)
+        h_transpose(0)
+        stay_warm()
+        h_multiply(1)
+        for q in range(4):
+            s_copy_out(1, q, "scalar")
+        h_transpose(1)
+        h_copy_out(0)
+        h_copy_out(1)
+        take_exp(2)
+        take_exp(3)
+        r_lay_out(r_parts[6], "vector", 0, 4)
+        r_quantize(r_parts[5])
+        r_lay_out(r_parts[7], "scalar", 0, 4)
+        stay_warm()
+        s_transpose(2, 0)
+        s_copy_out(2, 0, "scalar")
+        stay_warm()
+        h_quantize(0)
+        give_back(unread)
+        price_move(0)
+        h_multiply(2)
+        multiply_step = {i: 4 * (i // 2) - 5 + i % 2 for i in range(2, 8)}
+        steps = len(UNITS)
+        for step in range(steps + 1):
+            before = step - 1
+            short = step > steps - 2
+            relieve_scalar = step + 1 in (multiply_step[4], multiply_step[6])
+            if step >= 1:
+                width = UNITS[before][1]
+                y_transpose(before)
+                if not short:
+                    split = width if relieve_scalar else width * GPSIMD_SHARE // 16
+                    y_round(before, "gpsimd", 0, split)
+                    if split < width:
+                        y_round(before, "scalar", split, width)
+            if step < steps:
+                cost(step)
+            if step >= 1:
+                y_copy_out_and_store(before, "vector" if relieve_scalar else "scalar")
+            for i in range(2, 8):
+                if multiply_step[i] == step - 1:
+                    h_transpose(i)
+                    h_copy_out(i)
+            if step + 9 < 16:
+                s_transpose(*divmod(step + 9, 4))
+                s_copy_out(*divmod(step + 9, 4), "scalar")
+            for i in range(4, 8):
+                if multiply_step[i] == step + 1:
+                    take_exp(i)
+            if step + 1 < steps:
+                price_move(step + 1)
+            if short:
+                y_round(before, "vector", 0, width)
+            if step < 2:
+                r_quantize(r_parts[6 + step])
+            for i in range(3, 8):
+                if i % 2 == 1 and multiply_step[i] == step - 2:
+                    h_quantize(i // 2)
+                if multiply_step[i] == step:
+                    h_multiply(i)
+            if step >= 1:
+                y_quantize_and_store(before)
+            if before == 7:
+                store_scales(0, 2 * ROWS)
+        store_scales(2 * ROWS, M)

@@ -24,8 +24,7 @@ X_CHUNKS = ((0, 256), (256, 512), (512, 1024))
 UNITS = [(ROWS * r, ROWS, q) for r in range(4) for q in range(4)][:-1] + [(768, P, 3), (896, P, 3)]
 GPSIMD_SLOTS = 2
 GPSIMD_SHARE = 9
-HEAD_PASSES = (12, 8, 2)
-LONG_WAIT_PASSES = 6
+
 
 def tile_cube_root_impact_cost_h2_kernel(
     tc, flow_words, flow_scales, impact_words, impact_scales, depth_gain, response, drift, schedule,
@@ -81,18 +80,6 @@ def tile_cube_root_impact_cost_h2_kernel(
         zero = keep.tile([P, 1], F32, name="zero")
         nc.scalar.activation(out=zero[:], in_=ident[:, 0:1], func=ACT.Ln, scale=0.0, bias=1.0)
 
-        ones = keep.tile([P, W], BF16, name="ones", align_bytes=64)
-        ones_codes = keep.tile([P, P], U32, name="ones_codes", align_bytes=64)
-        ones_scales = keep.tile([P, P], U8, name="ones_scales", align_bytes=64)
-        nc.vector.memset(ones[:], 1.0)
-        nc.vector.quantize_mx(out=ones_codes[:].bitcast(FP8X4), scales=ones_scales[:], in_=ones[:])
-
-        def warm_up(bank, passes, rhs, rhs_scale, columns):
-            for repeat in range(passes):
-                nc.tensor.matmul_mx(
-                    out=bank[:, 0:columns], lhsT=ones_codes[:].bitcast(FP8X4), lhsT_scale=ones_scales[:],
-                    rhs=rhs, rhs_scale=rhs_scale, start=True, stop=True,
-                )
         g_words = []
         x_words = []
         r_raw = {}
@@ -381,12 +368,7 @@ def tile_cube_root_impact_cost_h2_kernel(
 
         r_parts = [(0, 0), (0, 1), (1, 0), (1, 1), (0, 2), (1, 2), (0, 3), (1, 3)]
         order = [(i, g) for g in range(2) for i in range(4)] + [(i, g) for i in range(4, 8) for g in range(2)]
-        unread = take_bank()
-        warm_up(unread, HEAD_PASSES[0], ones_codes[:].bitcast(FP8X4), ones_scales[:], P)
         spread_gain()
-        warm_up(unread, HEAD_PASSES[1], x_words[0][:, 0, 0:P].bitcast(FP8X4), ones_scales[:], P)
-        warm_up(unread, HEAD_PASSES[2], g_words[0][:, 0, :].bitcast(FP4X4), g_scales[0][:, 0, :], W)
-        give_back(unread)
         for n, (i, g) in enumerate(order):
             turn, position = divmod(n, 4)
             last_turn = turn == 3
@@ -405,25 +387,15 @@ def tile_cube_root_impact_cost_h2_kernel(
         take_log(*order[-1])
         load_s(3, 8)
 
-        unread = take_bank()
-
-        def stay_warm(passes=2):
-            warm_up(unread, passes, r_codes[:, 0, 0:W].bitcast(FP8X4), r_scales[:, 0, 0:W], W)
-
         for q in range(4):
             s_transpose(0, q)
             s_copy_out(0, q, "vector")
-            if q % 2 == 1:
-                stay_warm(LONG_WAIT_PASSES if q == 1 else 2)
         for q in range(4):
             s_transpose(1, q)
-            if q % 2 == 1:
-                stay_warm()
         take_exp(0)
         take_exp(1)
         h_multiply(0)
         h_transpose(0)
-        stay_warm()
         h_multiply(1)
         for q in range(4):
             s_copy_out(1, q, "scalar")
@@ -435,12 +407,9 @@ def tile_cube_root_impact_cost_h2_kernel(
         r_lay_out(r_parts[6], "vector", 0, 4)
         r_quantize(r_parts[5])
         r_lay_out(r_parts[7], "scalar", 0, 4)
-        stay_warm()
         s_transpose(2, 0)
         s_copy_out(2, 0, "scalar")
-        stay_warm()
         h_quantize(0)
-        give_back(unread)
         price_move(0)
         h_multiply(2)
         multiply_step = {i: 4 * (i // 2) - 5 + i % 2 for i in range(2, 8)}

from contextlib import ExitStack

import concourse.mybir as mybir
from concourse.masks import make_identity

M, K, A, N = 1024, 2048, 1024, 2048
FLOPS = 2 * M * K * A + 2 * M * A * N

F32 = mybir.dt.float32
BF16 = mybir.dt.bfloat16
I32 = mybir.dt.int32
U32 = mybir.dt.uint32
U8 = mybir.dt.uint8
FP8X4 = mybir.dt.float8_e4m3fn_x4
FP4X4 = mybir.dt.float4_e2m1fn_x4
ACT = mybir.ActivationFunctionType
ALU = mybir.AluOpType

P = 128
W = 512
ROWS = 256
LN_FLOOR = 2.0 ** -60
X_CHUNKS = ((0, 256), (256, 512), (512, 1024))
UNITS = [(ROWS * r, ROWS, q) for r in range(4) for q in range(4)][:-1] + [(768, P, 3), (896, P, 3)]
GPSIMD_SLOTS = 2
GPSIMD_SHARE = 9


def tile_cube_root_impact_cost_h2_kernel(
    tc, flow_words, flow_scales, impact_words, impact_scales, depth_gain, response, drift, schedule,
    out_0, out_1, out_2,
):
    nc = tc.nc
    with ExitStack() as ctx:
        keep = ctx.enter_context(tc.tile_pool(name="keep", bufs=1))
        ring = ctx.enter_context(tc.tile_pool(name="ring", bufs=2))
        psum = ctx.enter_context(tc.psum_pool(name="psum", bufs=1))
        ctx.enter_context(tc.manual_schedule())

        free_banks = list(range(8))
        banks_taken = []

        def take_bank():
            number = free_banks.pop(0)
            tile = psum.tile([P, W], F32, name="bank%d" % len(banks_taken), tag="bank%d" % number)
            banks_taken.append((tile, number))
            return tile

        def give_back(tile):
            free_banks.append([number for taken, number in banks_taken if taken is tile][0])

        def big(shape, dtype, place, name):
            return keep.tile(shape, dtype, name=name, tag="big%d" % place, align_bytes=64)

        def small(shape, dtype, place, name):
            return keep.tile(shape, dtype, name=name, tag="small%d" % place, align_bytes=64)

        def staging(shape, place, name):
            return keep.tile(shape, BF16, name=name, tag="staging%d" % place, align_bytes=64)

        def copy_on(engine, dst, src):
            if engine == "scalar":
                nc.scalar.copy(out=dst, in_=src)
            elif engine == "gpsimd":
                nc.gpsimd.tensor_scalar(out=dst, in0=src, scalar1=1.0, scalar2=0.0, op0=ALU.mult, op1=ALU.add)
            else:
                nc.vector.tensor_copy(out=dst, in_=src)

        x_scales = []
        g_scales = []
        for half in range(2):
            for planes, name in ((g_scales, "g_scales%d"), (x_scales, "x_scales%d")):
                plane = keep.tile([P, 4, W], U8, name=name % half, align_bytes=64)
                nc.vector.memset(plane[:].bitcast(I32), 0)
                planes.append(plane)
        gain_words = keep.tile([P, 2, 4], BF16, name="gain_words")
        nc.gpsimd.dma_start(out=gain_words[:], in_=depth_gain.rearrange("(g p t) -> p g t", g=2, t=4))
        ident = keep.tile([P, P], F32, name="ident")
        make_identity(nc, ident[:])
        zero = keep.tile([P, 1], F32, name="zero")
        nc.scalar.activation(out=zero[:], in_=ident[:, 0:1], func=ACT.Ln, scale=0.0, bias=1.0)

        g_words = []
        x_words = []
        r_raw = {}
        s_raw = {}

        def load_g(half):
            tile = small([P, 4, 2 * W], U8, half, "g_words%d" % half)
            cols = impact_words[:, :, 2 * W * half : 2 * W * (half + 1)]
            nc.sync.dma_start(out=tile[:].bitcast(I32), in_=cols.rearrange("g p b -> p g b").bitcast(I32))
            g_words.append(tile)

        def load_x(chunk):
            m0, m1 = X_CHUNKS[chunk]
            if m1 - m0 == W:
                tile = big([P, 4, W], U32, 8, "x_words%d" % chunk)
            else:
                tile = small([P, 4, m1 - m0], U32, 2 + chunk, "x_words%d" % chunk)
            cols = flow_words[:, :, m0:m1, :]
            nc.sync.dma_start(out=tile[:].bitcast(I32), in_=cols.rearrange("g p m t -> p g (m t)").bitcast(I32))
            x_words.append(tile)

        def load_scales(planes, scales, half, queues):
            for quad, queue in enumerate(queues):
                rows = scales[:, 4 * quad : 4 * quad + 4, W * half : W * (half + 1)]
                queue.dma_start(
                    out=planes[half][32 * quad : 32 * quad + 4, :, :].bitcast(I32),
                    in_=rows.rearrange("g r n -> r g n").bitcast(I32),
                )

        def load_r(g, half):
            r_raw[g, half] = big([P, 4, 2 * W], BF16, 9 + 2 * half + g, "r_raw%d%d" % (g, half))
            rows = response[W * g : W * (g + 1), 2 * W * half : 2 * W * (half + 1)]
            nc.sync.dma_start(out=r_raw[g, half][:], in_=rows.rearrange("(p j) n -> p j n", j=4))

        def load_s(r, place):
            s_raw[r] = big([P, 2, N], BF16, place, "s_raw%d" % r)
            rows = schedule[ROWS * r : ROWS * (r + 1), :]
            nc.sync.dma_start(out=s_raw[r][:], in_=rows.rearrange("(i p) n -> p i n", p=P))

        drift_words = keep.tile([P, 4, 4], BF16, name="drift_words")
        load_g(0)
        load_x(0)
        load_scales(g_scales, impact_scales, 0, [nc.sync] * 4)
        load_scales(x_scales, flow_scales, 0, [nc.sync] * 2 + [nc.gpsimd] * 2)
        load_x(1)
        load_g(1)
        load_scales(g_scales, impact_scales, 1, [nc.sync] * 4)
        load_r(0, 0)
        load_x(2)
        load_scales(x_scales, flow_scales, 1, [nc.sync] * 4)
        load_r(1, 0)
        load_r(0, 1)
        load_s(0, 13)
        load_r(1, 1)
        load_s(1, 14)
        nc.sync.dma_start(out=drift_words[:], in_=drift.rearrange("(q p t) -> p q t", q=4, t=4))
        load_s(2, 15)

        gain_all = keep.tile([P, A], BF16, name="gain_all")

        def spread_gain():
            bank = take_bank()
            pairs = gain_words[:].rearrange("p g t -> p (g t)").bitcast(F32)
            for c in range(4):
                nc.tensor.transpose(bank[:, P * c : P * (c + 1)], pairs[:, c : c + 1].to_broadcast([P, P]), ident[:])
            nc.vector.tensor_copy(out=gain_all[:].bitcast(F32), in_=bank[:])
            give_back(bank)

        power = {}
        u_gain = {}

        def by_pairs(cols):
            return cols.rearrange("m (u p e) -> m u p e", u=2, e=2)

        def pressure(i, g):
            chunk = [n for n, (m0, m1) in enumerate(X_CHUNKS) if m0 <= P * i < m1][0]
            col = P * i - X_CHUNKS[chunk][0]
            bank = take_bank()
            for k in range(4):
                nc.tensor.matmul_mx(
                    out=bank[:],
                    lhsT=x_words[chunk][:, k, col : col + P].bitcast(FP8X4),
                    lhsT_scale=x_scales[i // 4][:, k, P * (i % 4) : P * (i % 4 + 1)],
                    rhs=g_words[g][:, k, :].bitcast(FP4X4),
                    rhs_scale=g_scales[g][:, k, :],
                    start=(k == 0),
                    stop=(k == 3),
                )
            if g == 0:
                both = big([P, 2, A], F32, i, "power_and_u_gain%d" % i)
                power[i] = both[:, 0, :]
                u_gain[i] = both[:, 1, :]
            u_sorted = bank[:].rearrange("m (p u e) -> m u p e", u=2, e=2)
            cols = slice(W * g, W * (g + 1))
            nc.scalar.activation(out=by_pairs(power[i][:, cols]), in_=u_sorted, func=ACT.Abs, bias=zero[:])
            nc.vector.tensor_tensor(
                out=by_pairs(u_gain[i][:, cols]), in0=u_sorted, in1=by_pairs(gain_all[:, cols]), op=ALU.mult
            )
            give_back(bank)

        def take_log(i, g):
            part = power[i][:, W * g : W * (g + 1)]
            nc.scalar.activation(out=part, in_=part, func=ACT.Ln, bias=LN_FLOOR)

        def take_exp(i):
            nc.scalar.activation(out=power[i], in_=power[i], func=ACT.Exp, scale=-2.0 / 3.0)

        h_bf = {}
        h_banks = {}
        h_t = {}
        h_codes = keep.tile([P, 2, M], U32, name="h_codes", align_bytes=64)
        h_scales = keep.tile([P, 2, M], U8, name="h_scales", align_bytes=64)

        def h_multiply(i):
            h_bf[i] = ring.tile([P, A], BF16, name="h_bf%d" % i, tag="h_bf")
            nc.vector.tensor_tensor(out=h_bf[i][:], in0=u_gain[i], in1=power[i], op=ALU.mult)

        def h_transpose(i):
            h_banks[i] = take_bank()
            pairs = h_bf[i][:].bitcast(F32)
            for c in range(4):
                nc.tensor.transpose(h_banks[i][:, P * c : P * (c + 1)], pairs[:, P * c : P * (c + 1)], ident[:])

        def h_copy_out(i):
            r, which = divmod(i, 2)
            if which == 0:
                h_t[r] = staging([P, 2, ROWS, 4], 2 + r % 2, "h_t%d" % r)
            dst = h_t[r][:].bitcast(F32)[:, :, P * which : P * (which + 1), :]
            nc.scalar.copy(out=dst, in_=h_banks[i][:].rearrange("p (g u m) -> p g m u", u=2, m=P))
            give_back(h_banks[i])

        def h_quantize(r):
            for g in range(2):
                nc.vector.quantize_mx(
                    out=h_codes[:, g, ROWS * r : ROWS * (r + 1)].bitcast(FP8X4),
                    scales=h_scales[:, g, ROWS * r : ROWS * (r + 1)],
                    in_=h_t[r][:, g, :, :].rearrange("p m t -> p (m t)"),
                )

        r_codes = keep.tile([P, 2, N], U32, name="r_codes", align_bytes=64)
        r_scales = keep.tile([P, 2, N], U8, name="r_scales", align_bytes=64)
        r_laid = {}

        def r_lay_out(part, engine, t0, t1):
            g, q = part
            if part not in r_laid:
                r_laid[part] = staging([P, W, 4], len(r_laid) % 2, "r_laid%d%d" % part)
            src = r_raw[g, q // 2][:, :, W * (q % 2) : W * (q % 2 + 1)].rearrange("p j (c m t) -> p t c j m", m=2, t=4)
            dst = r_laid[part][:].rearrange("p (t c m) j -> p t c j m", t=4, m=2)
            if engine == "gpsimd":
                for t in range(t0, t1):
                    copy_on(engine, dst[:, t], src[:, t])
            else:
                copy_on(engine, dst[:, t0:t1], src[:, t0:t1])

        def r_quantize(part):
            g, q = part
            nc.vector.quantize_mx(
                out=r_codes[:, g, W * q : W * (q + 1)].bitcast(FP8X4),
                scales=r_scales[:, g, W * q : W * (q + 1)],
                in_=r_laid[part][:].rearrange("p n j -> p (n j)"),
            )

        s_banks = {}
        s_tiles = {}
        s_t = {}

        def s_transpose(r, q):
            s_banks[r, q] = take_bank()
            for u in range(2):
                for c in range(2):
                    pairs = s_raw[r][:, c, W * q : W * (q + 1)].bitcast(F32)
                    out = s_banks[r, q][:, P * (2 * u + c) : P * (2 * u + c + 1)]
                    nc.tensor.transpose(out, pairs[:, u : 2 * P : 2], ident[:])

        def s_copy_out(r, q, engine):
            if r < 2:
                if r == 0:
                    s_tiles["small", q] = small([P, 2, 2 * ROWS], F32, (q + 2) % 4, "s_t_small%d" % q)
                s_t[r, q] = s_tiles["small", q][:, :, ROWS * r : ROWS * (r + 1)]
            else:
                if q == 0:
                    s_tiles["big", r] = big([P, 4, 2, ROWS], F32, 7 + r, "s_t_big%d" % r)
                s_t[r, q] = s_tiles["big", r][:, q, :, :]
            copy_on(engine, s_t[r, q], s_banks[r, q][:].rearrange("p (u m) -> p u m", u=2))
            give_back(s_banks[r, q])

        d_banks = {}
        y_t = {}
        y_banks = {}
        y = {}
        y_bf = {}
        y_scales = keep.tile([P, M], U8, name="y_scales", align_bytes=64)
        y_places = (0, 1, 13, 14, 2, 3)
        y_tiles_made = []

        def y_tile(shape, name):
            y_tiles_made.append(name)
            return big(shape, F32, y_places[(len(y_tiles_made) - 1) % len(y_places)], name)

        def d_slot(unit, t):
            width = UNITS[unit][1]
            index, within = divmod(t, W // width)
            return d_banks[unit][index][:, width * within : width * (within + 1)]

        def price_move(unit):
            m0, width, q = UNITS[unit]
            d_banks[unit] = []
            for t in range(4):
                if t % (W // width) == 0:
                    d_banks[unit].append(take_bank())
                n0 = W * q + P * t
                for g in range(2):
                    nc.tensor.matmul_mx(
                        out=d_slot(unit, t),
                        lhsT=r_codes[:, g, n0 : n0 + P].bitcast(FP8X4),
                        lhsT_scale=r_scales[:, g, n0 : n0 + P],
                        rhs=h_codes[:, g, m0 : m0 + width].bitcast(FP8X4),
                        rhs_scale=h_scales[:, g, m0 : m0 + width],
                        start=(g == 0),
                        stop=(g == 1),
                    )

        def cost(unit):
            m0, width, q = UNITS[unit]
            r, first = divmod(m0, ROWS)
            y_t[unit] = y_tile([P, 4, width], "y_t%d" % unit)
            for t in range(4):
                u, e = divmod(t, 2)
                nc.vector.scalar_tensor_tensor(
                    out=y_t[unit][:, t, :],
                    in0=d_slot(unit, t),
                    scalar=drift_words[:, q, t : t + 1],
                    in1=s_t[r, q][:, u, first : first + width].bitcast(BF16)[:, e : 2 * width : 2],
                    op0=ALU.add,
                    op1=ALU.mult,
                )
            for bank in d_banks[unit]:
                give_back(bank)

        def y_transpose(unit):
            y_banks[unit] = []
            for i in range(UNITS[unit][1] // P):
                bank = take_bank()
                y_banks[unit].append(bank)
                for t in range(4):
                    nc.tensor.transpose(bank[:, P * t : P * (t + 1)], y_t[unit][:, t, P * i : P * (i + 1)], ident[:])

        def y_copy_out_and_store(unit, last_engine):
            m0, width, q = UNITS[unit]
            y[unit] = y_tile([P, width // P, W], "y%d" % unit)
            for i, bank in enumerate(y_banks[unit]):
                engine = last_engine if i == width // P - 1 else "scalar"
                dst = y[unit][:, i, :].rearrange("m (p t) -> m p t", t=4)
                copy_on(engine, dst, bank[:].rearrange("m (t p) -> m p t", t=4))
                give_back(bank)
            rows = out_0[m0 : m0 + width, W * q : W * (q + 1)]
            nc.sync.dma_start(out=rows.rearrange("(i p) n -> p i n", p=P), in_=y[unit][:])

        def y_round(unit, engine, c0, c1):
            if unit not in y_bf:
                y_bf[unit] = keep.tile([P, UNITS[unit][1], 4], BF16, name="y_bf%d" % unit, tag="y_bf", align_bytes=64)
            copy_on(
                engine,
                y_bf[unit][:, c0:c1, :].rearrange("p (c i) t -> p c t i", i=4),
                y_t[unit][:, :, c0:c1].rearrange("p t (c i) -> p c t i", i=4),
            )

        def y_quantize_and_store(unit):
            m0, width, q = UNITS[unit]
            codes = ring.tile([P, width], U32, name="y_codes%d" % unit, tag="y_codes", bufs=4, align_bytes=64)
            nc.vector.quantize_mx(
                out=codes[:].bitcast(FP8X4),
                scales=y_scales[4 * q : P, m0 : m0 + width],
                in_=y_bf[unit][:].rearrange("p m t -> p (m t)"),
            )
            words = out_1[q, :, m0 : m0 + width, :].rearrange("p m t -> p (m t)")
            nc.sync.dma_start(out=words.bitcast(I32), in_=codes[:].bitcast(I32))

        def store_scales(m0, m1):
            for quad in range(4):
                nc.sync.dma_start(
                    out=out_2[:, 4 * quad : 4 * quad + 4, m0:m1].bitcast(I32),
                    in_=y_scales[32 * quad : 32 * quad + 16, m0:m1].bitcast(I32),
                )

        r_parts = [(0, 0), (0, 1), (1, 0), (1, 1), (0, 2), (1, 2), (0, 3), (1, 3)]
        order = [(i, g) for g in range(2) for i in range(4)] + [(i, g) for i in range(4, 8) for g in range(2)]
        spread_gain()
        for n, (i, g) in enumerate(order):
            turn, position = divmod(n, 4)
            last_turn = turn == 3
            if position == 0 and turn > 0:
                r_lay_out(r_parts[2 * turn - 1], "gpsimd", 0, 4 if last_turn else GPSIMD_SLOTS)
            pressure(i, g)
            if n >= 1:
                take_log(*order[n - 1])
            if position == 3 and not last_turn:
                r_lay_out(r_parts[2 * turn], "vector", 0, 4)
                if turn > 0:
                    r_lay_out(r_parts[2 * turn - 1], "vector", GPSIMD_SLOTS, 4)
                r_quantize(r_parts[2 * turn])
                if turn > 0:
                    r_quantize(r_parts[2 * turn - 1])
        take_log(*order[-1])
        load_s(3, 8)

        for q in range(4):
            s_transpose(0, q)
            s_copy_out(0, q, "vector")
        for q in range(4):
            s_transpose(1, q)
        take_exp(0)
        take_exp(1)
        h_multiply(0)
        h_transpose(0)
        h_multiply(1)
        for q in range(4):
            s_copy_out(1, q, "scalar")
        h_transpose(1)
        h_copy_out(0)
        h_copy_out(1)
        take_exp(2)
        take_exp(3)
        r_lay_out(r_parts[6], "vector", 0, 4)
        r_quantize(r_parts[5])
        r_lay_out(r_parts[7], "scalar", 0, 4)
        s_transpose(2, 0)
        s_copy_out(2, 0, "scalar")
        h_quantize(0)
        price_move(0)
        h_multiply(2)
        multiply_step = {i: 4 * (i // 2) - 5 + i % 2 for i in range(2, 8)}
        steps = len(UNITS)
        for step in range(steps + 1):
            before = step - 1
            short = step > steps - 2
            relieve_scalar = step + 1 in (multiply_step[4], multiply_step[6])
            if step >= 1:
                width = UNITS[before][1]
                y_transpose(before)
                if not short:
                    split = width if relieve_scalar else width * GPSIMD_SHARE // 16
                    y_round(before, "gpsimd", 0, split)
                    if split < width:
                        y_round(before, "scalar", split, width)
            if step < steps:
                cost(step)
            if step >= 1:
                y_copy_out_and_store(before, "vector" if relieve_scalar else "scalar")
            for i in range(2, 8):
                if multiply_step[i] == step - 1:
                    h_transpose(i)
                    h_copy_out(i)
            if step + 9 < 16:
                s_transpose(*divmod(step + 9, 4))
                s_copy_out(*divmod(step + 9, 4), "scalar")
            for i in range(4, 8):
                if multiply_step[i] == step + 1:
                    take_exp(i)
            if step + 1 < steps:
                price_move(step + 1)
            if short:
                y_round(before, "vector", 0, width)
            if step < 2:
                r_quantize(r_parts[6 + step])
            for i in range(3, 8):
                if i % 2 == 1 and multiply_step[i] == step - 2:
                    h_quantize(i // 2)
                if multiply_step[i] == step:
                    h_multiply(i)
            if step >= 1:
                y_quantize_and_store(before)
            if before == 7:
                store_scales(0, 2 * ROWS)
        store_scales(2 * ROWS, M)
